import numpy as np, ml_dtypes
CORES = [10,34,74,98]
N = 4
BF = ml_dtypes.bfloat16
W, C, TS, S = 4096, 256, 6, 1
B = W // C
SHAPES = np.array([[0, 15, 1, 2, 3, 4, 5, 6, 7, 8, 9, 10, 11, 12, 13, 14], [0, 1, 2, 15, 3, 14, 4, 13, 5, 12, 6, 11, 7, 10, 8, 9], [14, 15, 0, 13, 1, 12, 2, 11, 3, 10, 4, 9, 5, 8, 6, 7],
                   [1, 14, 0, 15, 2, 3, 4, 5, 6, 7, 8, 9, 10, 11, 12, 13], [7, 8, 0, 15, 1, 14, 2, 13, 3, 12, 4, 11, 5, 10, 6, 9], [3, 11, 0, 8, 1, 9, 2, 10, 4, 12, 5, 13, 6, 14, 7, 15],
                   [0, 2, 1, 3, 4, 15, 5, 14, 6, 13, 7, 12, 8, 11, 9, 10]])
def place(a, b, n):
    return ((a * b >> 5) + 37 * a + 11 * b + (n & 63)) & (W - 1)
def mate(o):
    p = np.zeros_like(o); np.put_along_axis(p, o, o[..., np.array([0, 1, 3, 2, 5, 4, 7, 6, 9, 8, 11, 10, 13, 12, 15, 14])], -1)
    return np.ascontiguousarray(np.moveaxis(p, -1, -2))
def loose(p):
    m = p == np.arange(16).reshape(1, 1, 16, 1)
    return np.argmax(m, axis=2), 15 - np.argmax(m[:, :, ::-1], axis=2)
def look(x, l, p, fr, z, a):
    lf = np.take_along_axis(l, fr[:, :, None, :], 2); lp = np.take_along_axis(l, p, 2); n = a[:, :, None, None]
    xk = np.take_along_axis(x, place(l, lp, n).reshape(N, 8, 1, 16 * C), 3).reshape(N, 8, 16, 16, C)
    yk = np.take_along_axis(x, place(lf, l, n).reshape(N, 8, 1, 16 * C), 3).reshape(N, 8, 16, 16, C)
    dx = np.sum(np.abs(xk - z[:, :, :, None, :]), axis=2); dy = np.sum(np.abs(yk - z[:, :, :, None, :]), axis=2)
    return xk, yk, dx, dx - dy
def parts(rng):
    x = rng.integers(0, 64, (N, 8, 16, W)); l = rng.integers(0, 4096, (N, 8, 16, C)); z = rng.integers(0, 64, (N, 8, 16, C))
    p = mate(np.argsort(rng.random((N, 8, C, 16)), axis=-1)); t = rng.integers(60, 241, (N, 8, TS))
    return x, l, p, z, t
def pack(x, l, p, z, t):
    return {"xt": np.ascontiguousarray(x.reshape(N, 128, W)).astype(np.float32).astype(BF), "nm": np.ascontiguousarray(l.reshape(N, 128, C)).astype(np.int32),
            "pr": np.ascontiguousarray(p.reshape(N, 128, C)).astype(np.int32), "z0": np.ascontiguousarray(z.reshape(N, 128, C)).astype(np.float32).astype(BF),
            "th": np.ascontiguousarray(np.repeat(t, 16, axis=1)).astype(np.int32)}
def plant(rng, x, l, p, z, used, q, g, i, zz, v, w, odd, last):
    c = rng.integers(0, 4096, (512, 16)); pp = p[q, g, :, i]; bd = np.flatnonzero(pp != np.arange(16)); fr = int(np.flatnonzero(pp == np.arange(16))[0])
    hx = place(c[:, bd], c[:, pp[bd]], 0); hy = place(c[:, fr:fr + 1], c[:, bd], 0); h = np.concatenate([hx, hy], axis=1); k = np.sort(h, axis=1)
    fit = np.all(k[:, 1:] != k[:, :-1], axis=1) & ~np.any(used[h], axis=1); j = int(np.argmax(fit))
    assert fit[j], "no fitting names"
    ax = np.zeros((16, len(bd)), np.int64) + np.reshape(v, (-1, 1)); ax[15, :-1] = odd; ax[15, -1] = last
    xx = x[q, g]; xx[:, hx[j]] = ax; xx[:, hy[j]] = w
    l[q, g, :, i] = c[j]; z[q, g, :, i] = zz; used[h[j]] = True
def setup_inputs(rng):
    return pack(*parts(rng))
def setup_inputs_spread(rng):
    x, l, p, z, t = parts(rng)
    x = (rng.random((N, 8, 16, W)) * np.exp2(rng.integers(0, 7, (N, 8, 1, W)))).astype(np.int64); x = np.where(rng.random((N, 8, 1, W)) < 0.5, 63 - x, x)
    l = np.where(rng.random((N, 8, 1, C)) < 0.5, np.exp2(12 * rng.random((N, 8, 16, C))).astype(np.int64) - 1, l); l = np.minimum(l, 4095)
    z = np.where(rng.random((N, 8, 1, C)) < 0.7, np.minimum(np.exp2(6 * rng.random((N, 8, 16, C))).astype(np.int64) - 1, 63), z)
    t = np.where(rng.random((N, 8, TS)) < 0.4, rng.integers(-1008, 1009, (N, 8, TS)), rng.integers(0, 300, (N, 8, TS)))
    return pack(x, l, p, z, t)
def setup_inputs_ends(rng):
    x, l, p, z, t = parts(rng)
    x = 63 * np.where(rng.random((N, 8, 1, W)) < 0.75, rng.integers(0, 2, (N, 8, 1, W)), rng.integers(0, 2, (N, 8, 16, W)))
    l = np.where(rng.random((N, 8, 16, C)) < 0.75, 4095 * rng.integers(0, 2, (N, 8, 16, C)), l)
    z = 63 * np.where(rng.random((N, 8, 1, C)) < 0.6, rng.integers(0, 2, (N, 8, 1, C)), rng.integers(0, 2, (N, 8, 16, C)))
    sh = rng.integers(0, 6, (N, 8, C)); sh[:, :, np.array([0, C // 2, C - 1])] = 1
    sh[:, :, np.array([1, 2, C - 3])] = 6; sh[1::2, :, C // 2] = 6; p = mate(SHAPES[sh])
    t = 2016 * rng.integers(0, 2, (N, 8, TS)) - 1008; t[:, 0] = 1008; t[:, 1] = -1008
    t[:, 2] = rng.choice(np.array([1007, 0, -1007, 500]), (N, TS)); t[:, 5] = rng.choice(np.array([1007, 0, -1007, 500]), (N, TS))
    t[:, 2, 0] = 1007; t[:, 5, 0] = 1007; t[:, 7, 0] = 1007
    for q in range(N):
        for g in range(8):
            used = np.zeros(W, bool); m = int(rng.integers(9, 16))
            plant(rng, x, l, p, z, used, q, g, C - 1, 63, 0, 63, 1, 0)
            plant(rng, x, l, p, z, used, q, g, C - 2, 0, 0, 63, 0, 0)
            plant(rng, x, l, p, z, used, q, g, 0, 63, 63, 0, 62, 63)
            plant(rng, x, l, p, z, used, q, g, C // 2, 63, 0, 63, 0, 0)
            plant(rng, x, l, p, z, used, q, g, 1, 63, 0, 0, 0, 1)
            plant(rng, x, l, p, z, used, q, g, C - 3, 63, 63, 0, 63, 62)
            plant(rng, x, l, p, z, used, q, g, 2, 63, np.where(np.arange(16) < m, 0, 63), 0, 62, 63)
    return pack(x, l, p, z, t)
def setup_inputs_corners(rng):
    x, l, p, z, t = parts(rng); p = mate(SHAPES[rng.integers(0, 6, (N, 8, C))])
    l[:, 0] = rng.integers(0, 4096, (N, 1, C)); t[:, 0] = rng.integers(-1, 1, (N, TS))
    for q in range(N): l[q, 1] = (0, 4095, 1, 2048, 4094, 77, 1023, 64)[(q + int(rng.integers(0, 8))) % 8]
    l[:, 2] = 4095 * rng.integers(0, 2, (N, 16, C))
    x[:, 3] = rng.integers(0, 64, (N, 16, 1)); t[:, 3] = rng.integers(-1, 1, (N, TS))
    z[:, 4] = 63 * rng.integers(0, 2, (N, 1, C))
    t[:, 7] = 2016 * rng.integers(0, 2, (N, TS)) - 1008
    fr, e = loose(p); s = look(x, l, p, fr, z, np.zeros((N, 8), np.int64))[3]
    best = np.max(np.where(p != np.arange(16).reshape(1, 1, 16, 1), s, -1008), axis=2)
    t[:, 5, 0] = best[:, 5, 0]; t[:, 6, 0] = np.maximum(best[:, 6, C - 1] - 1, -1008)
    return pack(x, l, p, z, t)
def setup_inputs_crowd(rng):
    x, l, p, z, t = parts(rng); x = rng.integers(1, 63, (N, 8, 16, W)); z = rng.integers(1, 63, (N, 8, 16, C))
    l[:, 4] = rng.integers(0, 4096, (N, 1, 1)); l[:, 6] = rng.integers(0, 4096, (N, 1, 1))
    t[:] = 1008; t[:, 1, 0] = 1007; t[:, 5, 0] = 1007
    for g in (2, 3, 6, 7): t[:, g] = -1008
    for q in range(N):
        for g, i in ((1, C - 1), (5, 0)): plant(rng, x, l, p, z, np.zeros(W, bool), q, g, i, 63, 0, 63, 0, 0)
        for g, i in ((3, 0), (7, C - 1)): plant(rng, x, l, p, z, np.zeros(W, bool), q, g, i, 0, 0, 63, 0, 0)
    return pack(x, l, p, z, t)
def check_inputs(d):
    bad = []
    for k, lo, hi in (("xt", 0, 63), ("nm", 0, 4095), ("pr", 0, 15), ("z0", 0, 63), ("th", -1008, 1008)):
        v = np.asarray(d[k]).astype(np.float64)
        if not (np.min(v) >= lo and np.max(v) <= hi): bad.append("range of " + k)
        elif np.any(v != np.floor(v)): bad.append("whole numbers in " + k)
    p = np.clip(np.asarray(d["pr"]).astype(np.int64), 0, 15).reshape(N, 8, 16, C); row = np.arange(16).reshape(1, 1, 16, 1)
    if np.any(np.take_along_axis(p, p, 2) != row): bad.append("pairs in pr")
    if np.any(np.sum(p == row, axis=2) != 2): bad.append("two free rows in pr")
    t = np.asarray(d["th"]).reshape(N, 8, 16, TS)
    if np.any(t != t[:, :, :1]): bad.append("rows of a group alike in th")
    return bad
def reference(xt, nm, pr, z0, th):
    x = xt.astype(np.float32).astype(np.int64).reshape(N, 8, 16, W); l = nm.astype(np.int64).reshape(N, 8, 16, C); p = pr.astype(np.int64).reshape(N, 8, 16, C)
    z = z0.astype(np.float32).astype(np.int64).reshape(N, 8, 16, C); tt = th.astype(np.int64).reshape(N, 8, 16, TS)[:, :, 0]
    row = np.arange(16).reshape(1, 1, 16, 1); fr, e = loose(p); a = np.zeros((N, 8), np.int64); ct = np.zeros((TS, N, 8), np.int64)
    for t in range(TS):
        at = (np.arange(N) + S * t) % N; xa = x[at]
        xk, yk, dx, s = look(xa, l, p, fr, z, a[at]); bonded = p != row
        top = np.where(bonded, s, -9999); k1 = np.argmax(top, axis=2); k2 = np.argmin(np.where(bonded, dx, 9999), axis=2)
        esc = np.max(top, axis=2) <= tt[at][:, :, t:t + 1]
        k = np.where(esc, k2, k1); kk = k[:, :, None, :]; q = np.take_along_axis(p, kk, 2); es = esc[:, :, None, :]
        px = np.take_along_axis(xk, k[:, :, None, None, :], 3)[:, :, :, 0]; py = np.take_along_axis(yk, k[:, :, None, None, :], 3)[:, :, :, 0]
        z = np.where(es, np.abs(z - px), (z + py) >> 1)
        ff = fr[:, :, None, :]; m = np.where(es, e[:, :, None, :], kk)
        p = np.where(row == ff, m, np.where(row == m, ff, p)); p = np.where(row == q, q, p); p = np.where(es & (row == kk), kk, p)
        q = q[:, :, 0]; fr = np.where(esc, k, q); e = np.where(esc, q, e)
        col = (B * np.arange(C) + (np.sum(z, axis=2) & (B - 1)))[:, :, None, :]
        new = (np.take_along_axis(xa, col, 3) + z) >> 1
        np.put_along_axis(xa, np.ascontiguousarray(np.broadcast_to(col, (N, 8, 16, C))), new, 3); x[at] = xa
        ct[t, at] = np.sum(esc, axis=2); a = a + ct[t]
    return {"yx": x.reshape(N, 128, W).astype(np.float32).astype(BF), "ye": np.ascontiguousarray(np.repeat(np.moveaxis(ct, 0, -1), 16, axis=1)).astype(np.float32),
            "yp": p.reshape(N, 128, C).astype(np.float32), "yf": fr.astype(np.float32), "yz": z.reshape(N, 128, C).astype(np.float32).astype(BF)}

@@ -1,0 +1,605 @@
+import math
+from concourse.mybir import AluOpType, ActivationFunctionType
+
+ALU = AluOpType
+ACT = ActivationFunctionType
+TS, NR = 6, 4
+CH = 128
+NP = 112
+CX, CY = 17, 129
+WINW = 241 * 16
+M23 = 12582912.0
+M29 = 805306368.0
+XT = ["dddddddddddddd", "dddddddddddddd"]
+YT = ["ddddddddbbbbbb", "dddddddddbbbbb"]
+ON = {"nm": "VV", "z2": "SS", "zout": "SV", "t2": "VV", "rr": "VV", "zp": "VV", "na": "VV"}
+RANK = {"i": -7, "g": 1.5, "c": -6, "u": -10, "w": -6, "n": -4.0, "a1": -1, "l": 29, "G": 2, "f": 4, "d": 0.01}
+AB0 = 64.0 * 2880 - 13024
+SPLIT = True
+GS, RG = 7, 7
+
+_F, _I, _B, _U = {}, {}, {}, {}
+
+
+def _lay(tab, items):
+    n = 0
+    for name, w in items:
+        for c in (range(2) if name.endswith("_") else [None]):
+            tab[name if c is None else name + str(c)] = (n, w)
+            n += (w + 15) // 16 * 16
+    return n
+
+
+NF = _lay(_F, [("ix", 256), ("hi", 256), ("lo", 256), ("h16", 128), ("h64", 128), ("col", 16), ("yf32", 144), ("if32", 128), ("sw32", 128),
+               ("jj", 16), ("jt", 16), ("ctile", 8), ("e1", 256), ("e2", 256), ("qq_", 2048), ("bw_", 8), ("ye_", 8), ("cs_", 16), ("junk_", 8),
+               ("nm1_", 128), ("nm_", 128), ("na_", 224), ("n64_", 128), ("vk_", NP), ("ww_", NP), ("kk_", NP), ("t1_", 56), ("t2_", 32),
+               ("t3_", 16), ("mx_", 8), ("mxe_", 8), ("aa_", 8), ("fl_", 8), ("cu_", 8), ("gg_", 224), ("mm_", 224), ("dl_", 224), ("d1_", NP),
+               ("s1_", NP), ("id_", 128), ("sel_", 128), ("ta_", 128), ("wd_", 128), ("b1_", 128), ("b2_", 128), ("c2_", 128), ("q_", 128),
+               ("f16_", 128), ("pc_", 64), ("yp_", 128), ("yfo_", 128)])
+NI = _lay(_I, [("p", 2), ("k", 2), ("l8", 2), ("g48", 2), ("prod_", 224), ("sh_", 224), ("sm_", 224), ("base_", 224), ("m_", 8), ("cd_", 16),
+               ("o2_", 8), ("ui_", 8), ("u15_", 8), ("ti_", 128), ("fd_", 128), ("th_", 8)])
+NB = _lay(_B, [("yn", 144), ("yp", 144), ("id", 128), ("nid", 128), ("i4", 128), ("i8", 128), ("i7", 128), ("bm", 128), ("bm2", 128),
+               ("sw", 128), ("tri", 128), ("trt", 128), ("b0", 128), ("b1", 128), ("cx", NP), ("cy", NP), ("ci", 128), ("m192", 256), ("p8", 2),
+               ("lut", 768), ("lt", 512), ("frac_", 128), ("sg_", 8), ("t2_", 128), ("s_", 128), ("zp_", 128), ("xo_", 128), ("rr_", 256),
+               ("low_", 128), ("low8_", 128), ("free_", 128), ("ee_", 128), ("rw_", 128), ("xr_", 1792), ("ya_", 1792)])
+NU = _lay(_U, [("lbc", 8), ("lna", 14), ("lnb", 14), ("offs_", 224), ("o_", 16), ("c_", 16), ("fo_", 72)])
+
+SCRATCH = {
+    "X0": ("sbuf", [128, 4096], "bfloat16"), "X1": ("sbuf", [128, 4096], "bfloat16"),
+    "win0": ("sbuf", [128, WINW], "bfloat16"), "win1": ("sbuf", [128, WINW], "bfloat16"),
+    "nmi": ("sbuf", [128, 256], "int32"), "pri": ("sbuf", [128, 256], "int32"),
+    "zin": ("sbuf", [128, 7 * 256], "bfloat16"), "zout": ("sbuf", [128, 6 * 256], "bfloat16"),
+    "stin": ("sbuf", [128, 7 * 256], "float32"), "stout": ("sbuf", [128, 6 * 256], "float32"),
+    "FF": ("sbuf", [128, NF], "float32"), "II": ("sbuf", [128, NI], "int32"),
+    "BB": ("sbuf", [128, NB], "bfloat16"), "UU": ("sbuf", [128, NU], "uint16"),
+}
+BANKS = ("ps0", "ps1", "ps2", "pi", "pd", "pu0", "pu1", "pz")
+for _n in BANKS:
+    SCRATCH[_n] = ("psum", [128, 512], "float32")
+SEMAPHORES = (["cV", "cS", "cP", "cG", "sent"] + ["ar%d" % i for i in range(4 * TS)] + ["dm%d" % i for i in range(40)])
+
+CYC, PCY, GR, SR = 1.0, 0.5, 1.56, 3.5
+WAKE, RLAT, DLAT, DISS = 60.0, 3000.0, 2000.0, 80.0
+
+
+def build(g, core, T, topo):
+    rank = T.rank_of(core)
+    ops = []
+    rk = [-100]
+    bank = [0]
+
+    def R(name, lo, hi, step=1):
+        ap = T[name][:, lo:hi] if step == 1 else T[name][:, lo:hi:step]
+        ps = name in BANKS
+        wide = name not in ("X0", "X1", "win0", "win1", "zin", "zout", "BB", "UU")
+        return {"ap": ap, "keys": [(name, 0, 512)] if ps else [(name, lo, hi)], "n": len(range(lo, hi, step)), "ps": ps, "wide": wide, "ind": False}
+
+    def sub(tab, buf):
+        def f(name, lo=0, hi=None, step=1):
+            a, w = tab[name]
+            return R(buf, a + lo, a + (w if hi is None else hi), step)
+        return f
+    F, I, B, U = sub(_F, "FF"), sub(_I, "II"), sub(_B, "BB"), sub(_U, "UU")
+
+    def ind(win, off):
+        return {"ap": win["ap"].indirect(off["ap"]), "keys": win["keys"] + off["keys"], "wk": win["keys"], "ok": off["keys"],
+                "n": off["n"] * 16, "ps": False, "wide": True, "ind": True}
+
+    def add(q, fn, outs, ins, occ, lat=None, kind="c", sem=None, par=False):
+        rd, wr = [], []
+        for o in outs:
+            if o["ind"]:
+                wr += o["wk"]; rd += o["ok"]
+            else:
+                wr += o["keys"]
+        for o in ins:
+            if isinstance(o, dict):
+                if o["ps"]: wr += o["keys"]
+                else: rd += o["keys"]
+        ops.append({"q": q, "fn": fn, "rd": rd, "wr": wr, "occ": occ, "lat": occ if lat is None else lat, "kind": kind, "sem": sem,
+                    "rank": rk[0], "par": par})
+
+    A = lambda o: o["ap"] if isinstance(o, dict) else o
+
+    def vcost(out, in0, rate):
+        if out["ind"]: return 50 + SR * out["n"] * CYC
+        if in0["ind"]: return 50 + GR * in0["n"] * CYC
+        return max(64, rate * out["n"]) * CYC
+
+    def ts(out, in0, s1, s2, op0, op1=None):
+        rate = 1.0 if (out["wide"] or in0["wide"]) else 0.5
+        if op1 is None: fn = lambda: g.vector.tensor_scalar(A(out), A(in0), A(s1), None, op0)
+        else: fn = lambda: g.vector.tensor_scalar(A(out), A(in0), A(s1), A(s2), op0, op1)
+        add("V", fn, [out], [in0, s1, s2], vcost(out, in0, rate))
+
+    def tt(out, in0, in1, op):
+        rate = 1.0 if (in0["ps"] or in1["ps"]) else 2.0
+        add("V", lambda: g.vector.tensor_tensor(A(out), A(in0), A(in1), op), [out], [in0, in1], vcost(out, in0, rate))
+
+    def cp(out, in0):
+        rate = 1.0 if (out["wide"] or in0["wide"]) else 0.5
+        add("V", lambda: g.vector.tensor_copy(A(out), A(in0)), [out], [in0], vcost(out, in0, rate))
+
+    def ms(out, v):
+        add("V", lambda: g.vector.memset(A(out), v), [out], [], max(64, out["n"] * 0.5) * CYC)
+
+    def act(out, in0, func, bias=0.0, scale=1.0, acc=None):
+        c = 65 + GR * in0["n"] * CYC if in0["ind"] else max(64, in0["n"]) * CYC
+        if acc is None: fn = lambda: g.scalar.activation(A(out), A(in0), func, bias=A(bias), scale=A(scale))
+        else: fn = lambda: g.scalar.activation(A(out), A(in0), func, bias=A(bias), scale=A(scale), accum_out=A(acc))
+        add("S", fn, [out] + ([acc] if acc else []), [in0, bias, scale], c + (20 if acc else 0))
+
+    def lin(e, out, in0, scale, bias):
+        if e == "S": act(out, in0, ACT.Identity, bias=bias, scale=scale)
+        else: ts(out, in0, scale, bias, ALU.mult, ALU.add)
+
+    def mm(items):
+        def fn():
+            r = None
+            for o, l, x, st, sp in items:
+                r = g.tensor.matmul(o["ap"], l["ap"], x["ap"], st, sp)
+            return r
+        c = sum(max(64, x["n"]) * (4 if x["wide"] else 1) * PCY for o, l, x, st, sp in items)
+        add("P", fn, [it[0] for it in items], [it[1] for it in items] + [it[2] for it in items], c, c + 60)
+
+    def iota(out, pat, base, cm, flt=True):
+        if flt: fn = lambda: g.iota(A(out), pat, base, cm, allow_small_or_imprecise_dtypes=True)
+        else: fn = lambda: g.iota(A(out), pat, base, cm)
+        add("G", fn, [out], [], 130 + 2 * out["n"] * CYC)
+
+    nd = [0]
+
+    def dma(q, out, in0, outs, ins, nbytes, par=False):
+        sem = T.sem["dm%d" % nd[0]]; nd[0] += 1
+        e = g.sync if q == "Y" else g.scalar
+        add(q, lambda: e.dma_start(out, in0), outs, ins, DISS, DLAT + nbytes / 150.0, "d", (sem, 16), par)
+
+    def halves(reg):
+        name, lo, hi = reg["keys"][0]
+        return T[name][0:64, lo:hi], T[name][64:128, lo:hi]
+
+    def load2(qs, reg, src0, src1, nbytes):
+        a, b = halves(reg)
+        dma(qs[0], a, src0, [reg], [], nbytes)
+        dma(qs[1], b, src1, [reg], [], nbytes, True)
+
+    def store2(qs, dst, c, reg, nbytes):
+        a, b = halves(reg)
+        dma(qs[0], dst[64 * c:64 * c + 64, 0:CH], a, [], [reg], nbytes)
+        dma(qs[1], dst[64 * c:64 * c + 64, CH:2 * CH], b, [], [reg], nbytes)
+
+    na = [0]
+
+    def send(dst, src, to):
+        sem = T.sem["ar%d" % na[0]]; na[0] += 1
+        peer = T.cores[to % NR]
+        rid, pid, se = topo.addr(peer)
+        mask = topo.mask(core, peer)
+        ne = len(topo.engines(core, peer))
+        add("G", lambda: g.remote_dma(dst["ap"], src["ap"], sem, T.sem.sent, pid, rid, mask), [dst], [src], 150, RLAT, "r", (sem, ne))
+
+    col = lambda j: F("col", j, j + 1)
+    PCOL, KCOL, G15, G16, L8, K16, LT8, GE8, P8, G48, P64, H2K = [col(j) for j in range(12)]
+    seln = lambda i: B("yn", 15 - i, 143 - i)
+    selp = lambda i: B("yp", 15 - i, 143 - i)
+    self32 = lambda i: F("yf32", 15 - i, 143 - i)
+    zin = lambda t, c: R("zin", (2 * t + c) * CH, (2 * t + c + 1) * CH)
+    zout = lambda t, c: R("zout", (2 * t + c) * CH, (2 * t + c + 1) * CH)
+    stin = lambda t, c, lo=0, hi=CH: R("stin", (2 * t + c) * CH + lo, (2 * t + c) * CH + hi)
+    stout = lambda t, c, lo=0, hi=CH: R("stout", (2 * t + c) * CH + lo, (2 * t + c) * CH + hi)
+    ix = lambda lo, hi: F("ix", lo, hi)
+    XW = lambda c: R("X%d" % c, 0, 4096)
+    cs = lambda c, j: F("cs_%d" % c, j, j + 1)
+
+    for c in range(2):
+        rk[0] = -100 + c
+        rows = slice(64 * c, 64 * c + 64); qs = "YS" if c == 0 else "YY"
+        load2(qs, R("pri", c * CH, (c + 1) * CH), T.pr[rows, 0:CH], T.pr[rows, CH:2 * CH], 32768)
+        load2(qs, R("nmi", c * CH, (c + 1) * CH), T.nm[rows, 0:CH], T.nm[rows, CH:2 * CH], 32768)
+        load2(qs, XW(c), T.xt[rows, :], T.xt[rows, :], 1048576 * (c + 1))
+        load2("YY", zin(0, c), T.z0[rows, 0:CH], T.z0[rows, CH:2 * CH], 16384)
+        load2("YY", I("th_%d" % c, 0, 6), T.th[rows, :], T.th[rows, :], 1536)
+
+    rk[0] = -100
+    iota(I("p", 0, 1), [[0, 1]], 0, 1, False)
+    iota(F("ix"), [[1, 256]], 0, 0)
+    iota(F("h16"), [[16, 8], [0, 16]], 0, 0)
+    iota(B("ci"), [[240, 16], [0, 8]], 240, 0)
+    ts(I("k", 0, 1), I("p", 0, 1), 15, None, ALU.bitwise_and)
+    cp(PCOL, I("p", 0, 1)); cp(KCOL, I("k", 0, 1))
+    tt(G16, PCOL, KCOL, ALU.subtract)
+    ts(G15, G16, 15.0, None, ALU.add)
+    ts(LT8, KCOL, 8.0, None, ALU.is_lt)
+    ts(GE8, KCOL, 8.0, None, ALU.is_ge)
+    act(B("p8", 0, 1), KCOL, ACT.Exp, bias=-16.0 * math.log(2.0), scale=math.log(8.0))
+    act(P8, B("p8", 0, 1), ACT.Identity)
+    ts(B("bm"), F("h16"), G16, None, ALU.is_equal)
+    ts(B("trt"), ix(0, 128), PCOL, 65536.0, ALU.is_gt, ALU.mult)
+    tt(B("tri"), B("trt"), B("bm"), ALU.mult)
+    ts(B("b0"), B("bm"), LT8, None, ALU.mult)
+    ts(B("b1"), B("bm"), GE8, None, ALU.mult)
+    ts(B("id"), ix(0, 128), PCOL, None, ALU.is_equal)
+    for name, v in (("i7", 458752.0), ("i4", -4096.0)):
+        act(B(name), B("id"), ACT.Identity, scale=v)
+    ts(F("yf32"), ix(0, 144), G15, None, ALU.is_equal)
+    rk[0] = -40
+    iota(F("h64"), [[0, 2], [16, 4], [0, 16]], 0, 0)
+    iota(F("hi"), [[1, 16], [0, 16]], 0, 0)
+    iota(F("lo"), [[0, 16], [1, 16]], 0, 0)
+    for name, v in (("nid", -1.0), ("i8", -8192.0)):
+        act(B(name), B("id"), ACT.Identity, scale=v)
+    act(F("if32"), B("id"), ACT.Identity)
+    act(B("yn"), F("yf32"), ACT.Identity, scale=-2048.0)
+    act(B("yp"), F("yf32"), ACT.Identity, scale=4096.0)
+    ts(I("l8", 0, 1), I("p", 0, 1), 7, None, ALU.bitwise_and)
+    ts(I("g48", 0, 1), I("p", 0, 1), 48, None, ALU.bitwise_and)
+    cp(L8, I("l8", 0, 1)); cp(G48, I("g48", 0, 1))
+    ts(U("lbc"), ix(0, 8), 0.0, L8, ALU.mult, ALU.add)
+    act(B("cx"), ix(0, NP), ACT.Identity, bias=float(CX))
+    act(B("cy"), ix(0, NP), ACT.Identity, bias=float(CY))
+    for c in range(2):
+        ms(F("cs_%d" % c, 5, 6), AB0)
+        ms(R("win%d" % c, 0, 272), 128.0)
+    rk[0] = -1
+    ts(H2K, PCOL, 64.0, 2048.0, ALU.is_ge, ALU.mult)
+    act(K16, KCOL, ACT.Identity, bias=H2K, scale=16.0)
+    ts(F("ctile"), ix(0, 8), 256.0, K16, ALU.mult, ALU.add)
+    ts(B("bm2"), F("h64"), G48, None, ALU.is_equal)
+    act(P64, H2K, ACT.Identity, bias=PCOL, scale=-1.0 / 16)
+    ts(F("sw32"), ix(0, 128), -64.0, P64, ALU.add, ALU.is_equal)
+    act(B("sw"), F("sw32"), ACT.Identity)
+    for c in range(2):
+        ts(F("bw_%d" % c, 0, 6), I("th_%d" % c, 0, 6), -4096.0, -2176.0, ALU.mult, ALU.add)
+    ms(B("m192"), -192.0)
+
+    def arrange(c):
+        s = str(c)
+        pr = R("pri", c * CH, (c + 1) * CH); nm = R("nmi", c * CH, (c + 1) * CH)
+        if c == 0: pa, pb, w0, w1, po = R("ps0", 0, 128), R("ps1", 0, 128), R("ps2", 0, 128), R("pd", 0, 128), "pu0"
+        else: pa, pb, w0, w1, po = R("pz", 0, 128), R("pu1", 128, 256), R("pz", 128, 256), R("pz", 256, 384), "pu1"
+        ts(B("low_" + s), pr, KCOL, None, ALU.is_gt)
+        ts(B("low8_" + s), pr, KCOL, P8, ALU.is_gt, ALU.mult)
+        ts(B("free_" + s), pr, KCOL, None, ALU.is_equal)
+        ts(F("id_" + s), pr, KCOL, None, ALU.min)
+        mm([(pa, B("tri"), B("low_" + s), True, True)])
+        tt(B("rw_" + s), pa, B("low8_" + s), ALU.mult)
+        mm([(pb, B("tri"), B("free_" + s), True, False), (pb, B("i7"), B("free_" + s), False, True)])
+        ts(F("sel_" + s), F("id_" + s), 8.0, None, ALU.is_ge)
+        act(B("ee_" + s), F("id_" + s), ACT.Exp, bias=math.log(8.0), scale=-math.log(8.0))
+        mm([(w1, B("b1"), B("rw_" + s), True, True)])
+        mm([(w0, B("b0"), B("rw_" + s), True, True)])
+        tt(F("ta_" + s), w1, F("sel_" + s), ALU.mult)
+        tt(F("wd_" + s), w0, F("ta_" + s), ALU.add)
+        tt(I("ti_" + s), F("wd_" + s), B("ee_" + s), ALU.mult)
+        ts(I("fd_" + s), I("ti_" + s), 3, 7, ALU.arith_shift_right, ALU.bitwise_and)
+        ts(F("b1_" + s), nm, 16.0, KCOL, ALU.mult, ALU.add)
+        ts(F("c2_" + s), pr, KCOL, 458752.0, ALU.is_le, ALU.mult)
+        tt(F("b2_" + s), pb, B("free_" + s), ALU.mult)
+        tt(F("b1_" + s), F("b1_" + s), F("c2_" + s), ALU.add)
+        tt(F("b2_" + s), F("b2_" + s), F("b1_" + s), ALU.add)
+        ts(F("q_" + s), I("fd_" + s), 65536.0, None, ALU.mult)
+        tt(F("q_" + s), F("q_" + s), F("b2_" + s), ALU.add)
+        mm([(R(po, 0, 128), B("i4"), B("ci"), True, False)])
+        for h in range(2):
+            for p in range(8 * h, 8 * h + 8):
+                ts(F("qq_" + s, p * CH, (p + 1) * CH), F("q_" + s), 65536.0 * p, 65536.0 * (p + 1), ALU.max, ALU.min)
+            for i0 in range(0, 16, 2):
+                mm([(R(po, 64 * h, 64 * h + 64), self32(i), F("qq_" + s, 1024 * h + i, 1024 * (h + 1), 16), False, h == 1 and i == 15)
+                    for i in range(i0, i0 + 2)])
+        act(stin(0, c), R(po, 0, 128), ACT.Identity, bias=-1696.0 - 15.0 / 32, scale=1.0 / 16)
+
+    def unpack(t, c, n):
+        s = str(c)
+        if ON["nm"][c] == "S":
+            act(F("nm1_" + s), stin(t, c), ACT.Identity, bias=M23)
+            act(F("nm_" + s), F("nm1_" + s), ACT.Identity, bias=-M23)
+        else:
+            ts(F("nm_" + s), stin(t, c), M23, -M23, ALU.add, ALU.add)
+        tt(B("frac_" + s, 0, n), stin(t, c, 0, n), F("nm_" + s, 0, n), ALU.subtract)
+
+    def index(t, c):
+        s = str(c); wn = "win" + s
+        unpack(t, c, NP)
+        nm = lambda a, b: F("nm_" + s, a, b)
+        for h in range(2):
+            act(R("pi", 56 * h, 56 * h + 56), nm(56 - 56 * h, NP - 56 * h), ACT.Identity, bias=2880.0)
+        tt(I("prod_" + s, 0, NP), R("pi", 0, NP), nm(0, NP), ALU.mult)
+        if ON["na"][c] == "S":
+            act(F("na_" + s, 0, NP), ind(nm(112, 120), U("lbc", 0, 7)), ACT.Copy)
+            tt(I("prod_" + s, NP, 224), R("pi", 0, NP), F("na_" + s, 0, NP), ALU.mult)
+        else:
+            for h in range(2):
+                act(F("na_" + s, 56 * h, 56 * h + 56), nm(56 - 56 * h, NP - 56 * h), ACT.Identity, bias=2880.0)
+            tt(I("prod_" + s, NP, 224), ind(nm(112, 120), U("lbc", 0, 7)), F("na_" + s, 0, NP), ALU.mult)
+        for h in range(2):
+            act(R("pi", 128 + 56 * h, 184 + 56 * h), nm(56 - 56 * h, NP - 56 * h), ACT.Identity, bias=cs(c, 5), scale=64.0)
+        parts = ((0, NP), (NP, 224)) if SPLIT else ((0, 224),)
+        for a, b in parts:
+            ts(I("sh_" + s, a, b), I("prod_" + s, a, b), 5, None, ALU.arith_shift_right)
+            for a1 in range(a, b, NP):
+                tt(I("sm_" + s, a1, a1 + NP), R("pi", 128, 128 + NP), I("sh_" + s, a1, a1 + NP), ALU.add)
+            ts(I("base_" + s, a, b), I("sm_" + s, a, b), 4095, None, ALU.bitwise_and)
+            cp(U("offs_" + s, a, b), I("base_" + s, a, b))
+        rk[0] = 10 * t + 5 * c + RANK["G"]
+        tt(F("gg_" + s, 0, 224, 2), ind(stin(t, c, 112, 120), U("lbc", 0, 7)), stin(t, c, 0, NP), ALU.subtract)
+        tt(F("gg_" + s, 1, 224, 2), ind(stin(t, c, 120, 128), U("lbc", 0, 7)), stin(t, c, 0, NP), ALU.subtract)
+        if YT[c].count("d") < 14: lin(ON["z2"][c], R(wn, 16, 144), zin(t, c), 2.0, 128.0)
+        if "d" in YT[c]: lin(ON["z2"][c], R(wn, 144, 272), zin(t, c), 1.0, 128.0)
+
+    def runs(types, ch, most, lo, hi):
+        out, j = [], lo
+        while j < hi:
+            if types[j] in ch:
+                e = j
+                while e < hi and types[e] == types[j] and e - j < most: e += 1
+                out.append((j, e)); j = e
+            else:
+                j += 1
+        return out
+
+    def gathers(t, c):
+        s = str(c); wn = "win" + s; pu = "pu" + s
+        xt, yt = XT[c], YT[c]
+        Xw = XW(c); z = zin(t, c)
+        off = lambda ty, a, b: U("offs_" + s, ty * NP + 8 * a, ty * NP + 8 * b)
+        wx = lambda a, b, st=1, i=0: R(wn, CX * 16 + a * CH + i, CX * 16 + b * CH, st)
+        wy = lambda a, b, st=1, i=0: R(wn, CY * 16 + a * CH + i, CY * 16 + b * CH, st)
+        xr = lambda a, b: B("xr_" + s, a * CH, b * CH)
+        ya = lambda a, b, st=1, i=0: B("ya_" + s, a * CH + i, b * CH, st)
+
+        def dblock(ty, a, b, raw, dst):
+            rk[0] += RANK["d"]
+            act(raw(a, b), ind(Xw, off(ty, a, b)), ACT.Copy)
+            for a1 in range(a, b, 4):
+                b1 = min(b, a1 + 4)
+                pb = "ps%d" % (bank[0] % 3); bank[0] += 1
+                mm([(R(pb, 0, (b1 - a1) * CH), B("id"), raw(a1, b1), True, False)] +
+                   [(R(pb, j * CH, (j + 1) * CH), B("nid"), z, False, j == b1 - a1 - 1) for j in range(b1 - a1)])
+                act(dst(a1, b1), R(pb, 0, (b1 - a1) * CH), ACT.Abs, scale=2.0)
+        mm([(R("pd", 0, NP), B("id"), B("cx"), True, False), (R("pd", 0, NP), B("i4"), B("frac_" + s, 0, NP), False, False)])
+        mm([(R(pu, 0, NP), B("id"), B("cy"), True, False),
+            (R(pu, 0, 56), B("id"), B("cx", 56, NP), False, False), (R(pu, 56, NP), B("id"), B("cx", 0, 56), False, False),
+            (R(pu, 0, 56), B("i8"), B("frac_" + s, 56, NP), False, False), (R(pu, 56, NP), B("i8"), B("frac_" + s, 0, 56), False, False)])
+        for lo in range(0, 14, RG):
+            hi = lo + RG
+            for a, b in runs(xt, "d", GS, lo, hi): dblock(0, a, b, xr, wx)
+            for a, b in runs(xt, "b", 7, lo, hi):
+                for j in range(a, b): tt(xr(j, j + 1), ind(Xw, off(0, j, j + 1)), z, ALU.subtract)
+                act(wx(a, b), xr(a, b), ACT.Abs, scale=2.0)
+            mm([(R("pd", 8 * lo, 8 * hi), seln(i), wx(lo, hi, 16, i), False, hi == 14 and i == 15) for i in range(16)])
+        act(F("ww_" + s), R("pd", 0, NP), ACT.Identity, bias=F("bw_" + s, t, t + 1), scale=-1.0)
+        act(F("vk_" + s), R("pd", 0, NP), ACT.Identity, bias=4130688.0 / 16777216.0, scale=1.0 / 16777216.0)
+        for lo in range(0, 14, RG):
+            hi = lo + RG
+            for a, b in runs(yt, "d", GS, lo, hi): dblock(1, a, b, wy, ya)
+            for a, b in runs(yt, "ab", 7, lo, hi):
+                for j in range(a, b): tt(wy(j, j + 1), ind(Xw, off(1, j, j + 1)), z, ALU.subtract)
+                if yt[a] == "a": ts(ya(a, b), wy(a, b), 0.0, 4.0, ALU.max, ALU.mult)
+                else: act(ya(a, b), wy(a, b), ACT.Abs, scale=2.0)
+            for a, b in runs(yt, "a", 14, lo, hi):
+                mm([(R(pu, 8 * a, 8 * b), selp(i), wy(a, b, 16, i), False, False) for i in range(16)])
+            if hi == 14:
+                mm([(R(pu, 0, 56), F("if32"), F("ww_" + s, 56, NP), False, False), (R(pu, 56, NP), F("if32"), F("ww_" + s, 0, 56), False, False)])
+            mm([(R(pu, 8 * lo, 8 * hi), seln(i), ya(lo, hi, 16, i), False, hi == 14 and i == 15) for i in range(16)])
+
+    def choose(t, c):
+        s = str(c); wn = "win" + s
+        K = lambda a=0, b=NP: F("kk_" + s, a, b)
+        mx = F("mx_" + s)
+        tt(K(), R("pu" + s, 0, NP), F("vk_" + s), ALU.max)
+        tt(F("t1_" + s), K(0, 56), K(56, NP), ALU.max)
+        tt(F("t2_" + s), F("t1_" + s, 0, 32), F("t1_" + s, 24, 56), ALU.max)
+        tt(F("t3_" + s), F("t2_" + s, 0, 16), F("t2_" + s, 16, 32), ALU.max)
+        tt(mx, F("t3_" + s, 0, 8), F("t3_" + s, 8, 16), ALU.max)
+        rk[0] = 10 * t + 5 * c + RANK["n"]
+        count(t, c)
+        rk[0] = 10 * t + 5 * c + RANK["u"]
+        update(t, c)
+        rk[0] = 10 * t + 5 * c + RANK["c"]
+        ts(F("aa_" + s), mx, 16777216.0, 4194304.0, ALU.mult, ALU.min)
+        tt(I("m_" + s), F("aa_" + s), mx, ALU.add)
+        ts(I("cd_" + s, 0, 8), I("m_" + s), 255, None, ALU.bitwise_and)
+        nd_ = YT[c].count("d")
+        if nd_ == 14:
+            tt(I("cd_" + s, 8, 16), mx, ix(9, 17), ALU.min)
+        elif nd_:
+            tt(I("o2_" + s), mx, ix(9, 17), ALU.min)
+            ts(F("fl_" + s), I("cd_" + s, 0, 8), float(CY + 8 * nd_), -8.0, ALU.is_ge, ALU.mult)
+            tt(I("cd_" + s, 8, 16), I("o2_" + s), F("fl_" + s), ALU.add)
+        else:
+            tt(I("cd_" + s, 8, 16), mx, ix(1, 9), ALU.min)
+        ts(U("o_" + s), I("cd_" + s), 16.0, KCOL, ALU.mult, ALU.add)
+        if ON["t2"][c] == "S": act(B("t2_" + s), ind(R(wn, 0, 272), U("o_" + s, 8, 16)), ACT.Copy)
+        else: cp(B("t2_" + s), ind(R(wn, 0, 272), U("o_" + s, 8, 16)))
+        tt(B("s_" + s), ind(R(wn, 0, WINW), U("o_" + s, 0, 8)), B("t2_" + s), ALU.add)
+        lin(ON["zp"][c], B("zp_" + s), B("s_" + s), 0.5, 63.875)
+        lin(ON["zout"][c], zout(t, c), B("zp_" + s), 1.0, -128.0)
+        send(zin(t + 1, c), zout(t, c), rank + 1 if t < TS - 1 else rank - (TS - 1))
+        rk[0] = 10 * t + 5 * c + RANK["w"]
+        mm([(R("pz", 0, 8), selp(i), B("zp_" + s, i, CH, 16), i == 0, i == 15) for i in range(16)])
+        ts(I("ui_" + s), R("pz", 0, 8), 1.0 / 4096, None, ALU.mult)
+        ts(I("u15_" + s), I("ui_" + s), 15, None, ALU.bitwise_and)
+        tt(F("cu_" + s), I("u15_" + s), F("ctile"), ALU.add)
+        cp(U("c_" + s, 0, 8), F("cu_" + s))
+        tt(B("xo_" + s), ind(XW(c), U("c_" + s, 0, 8)), B("zp_" + s), ALU.add)
+        lin(ON["rr"][c], B("rr_" + s, 0, CH), B("xo_" + s), 0.5, 127.875)
+        mm([(R("pz", 8, 16), F("sw32"), F("cu_" + s), True, True)])
+        cp(U("c_" + s, 8, 16), R("pz", 8, 16))
+        mm([(R("pz", 128, 256), B("sw"), B("rr_" + s, 0, CH), True, True)])
+        act(B("rr_" + s, CH, 2 * CH), R("pz", 128, 256), ACT.Identity)
+        tt(ind(XW(c), U("c_" + s)), B("rr_" + s), B("m192"), ALU.add)
+        if t == TS - 1:
+            x = T["X" + s]
+            dma("Y", T.yx[64 * c:64 * c + 64, 0:2048], x[0:64, 0:2048], [], [XW(c)], 524288)
+            dma("S" if c else "Y", T.yx[64 * c:64 * c + 64, 2048:4096], x[64:128, 2048:4096], [], [XW(c)], 524288)
+
+    def update(t, c):
+        s = str(c); mx = F("mx_" + s); K = F("kk_" + s)
+        ts(F("mxe_" + s), mx, 0.5, None, ALU.min)
+        tt(F("mm_" + s, 0, NP), ind(mx, U("lbc", 0, 7)), K, ALU.is_equal)
+        tt(F("s1_" + s), ind(F("mxe_" + s), U("lbc", 0, 7)), K, ALU.is_equal)
+        dl = lambda a, b, st=1: F("dl_" + s, a, b, st)
+        tt(dl(0, 224, 2), F("mm_" + s, 0, NP), F("gg_" + s, 0, 224, 2), ALU.mult)
+        tt(dl(1, 112, 2), F("s1_" + s, 56, NP), F("gg_" + s, 1, 112, 2), ALU.mult)
+        tt(dl(113, 224, 2), F("s1_" + s, 0, 56), F("gg_" + s, 113, 224, 2), ALU.mult)
+        d1 = lambda a, b, st=1: F("d1_" + s, a, b, st)
+        tt(d1(0, 112), dl(0, 112), dl(112, 224), ALU.add)
+        tt(d1(0, 48), d1(0, 48), d1(64, 112), ALU.add)
+        tt(d1(0, 32), d1(0, 32), d1(32, 64), ALU.add)
+        tt(d1(0, 16), d1(0, 16), d1(16, 32), ALU.add)
+        tt(stout(t, c, 112, 120), stin(t, c, 112, 120), d1(0, 16, 2), ALU.subtract)
+        tt(stout(t, c, 120, 128), stin(t, c, 120, 128), d1(1, 16, 2), ALU.subtract)
+        tt(F("s1_" + s), stin(t, c, 0, NP), dl(0, 224, 2), ALU.add)
+        tt(stout(t, c, 0, NP), F("s1_" + s), dl(1, 224, 2), ALU.add)
+        send(stin(t + 1, c), stout(t, c), rank + 1 if t < TS - 1 else rank - (TS - 1))
+
+    def count(t, c):
+        s = str(c)
+        TC, R1, NRR, AN, BT, AB = [cs(c, j) for j in range(6)]
+        pc = R("pz", 16, 24)
+        act(B("sg_" + s), F("mx_" + s), ACT.Sign, bias=-0.5)
+        mm([(pc, B("bm2"), B("sg_" + s), True, True)])
+        act(F("junk_" + s), pc, ACT.Identity, bias=16.0, scale=-0.5, acc=F("ye_" + s, t, t + 1))
+        if t < TS - 1:
+            ts(TC, F("ye_" + s, t, t + 1), AB, -31.5 - AB0, ALU.add, ALU.add)
+            ts(R1, TC, M29, -M29, ALU.add, ALU.add)
+            ts(AB, TC, R1, 31.5 + AB0, ALU.subtract, ALU.add)
+        else:
+            a = _F["ye_" + s][0]
+            dma("Y", T.ye[64 * c:64 * c + 64, :], T.FF[0:64, a:a + TS], [], [F("ye_" + s)], 1536)
+
+    def lut():
+        ts(F("e1"), F("hi"), KCOL, None, ALU.is_equal)
+        ts(F("e2"), F("lo"), KCOL, None, ALU.is_equal)
+        tt(B("lt", 0, 256), F("e1"), F("lo"), ALU.mult)
+        tt(B("lt", 256, 512), F("e2"), F("hi"), ALU.mult)
+        tt(B("lut", 0, 256), B("lt", 0, 256), B("lt", 256, 512), ALU.add)
+        tt(B("lt", 0, 256), F("e1"), F("e2"), ALU.add)
+        ts(B("lut", 256, 512), B("lt", 0, 256), KCOL, None, ALU.mult)
+        act(B("lut", 512, 768), F("hi"), ACT.Identity)
+
+    def finish(c):
+        s = str(c)
+        store2("YY", T.yz, c, zin(TS, c), 16384)
+        unpack(TS, c, CH)
+        act(F("f16_" + s), B("frac_" + s), ACT.Identity, scale=16.0)
+        tt(F("pc_" + s, 0, 56), F("f16_" + s, 0, 56), B("frac_" + s, 56, NP), ALU.add)
+        tt(F("pc_" + s, 56, 64), F("f16_" + s, 112, 120), B("frac_" + s, 120, 128), ALU.add)
+        ts(U("fo_" + s, 0, 56), F("pc_" + s, 0, 56), 16.0, 127.5, ALU.mult, ALU.add)
+        ts(U("fo_" + s, 56, 64), F("pc_" + s, 56, 64), 16.0, 383.5, ALU.mult, ALU.add)
+        ts(U("fo_" + s, 64, 72), F("pc_" + s, 56, 64), 16.0, 639.5, ALU.mult, ALU.add)
+        L = B("lut")
+        cp(B("xr_" + s, 0, 512), ind(L, U("fo_" + s, 0, 32)))
+        act(B("xr_" + s, 512, 1024), ind(L, U("fo_" + s, 32, 64)), ACT.Copy)
+        cp(F("yfo_" + s), ind(L, U("fo_" + s, 64, 72)))
+        pb = R("pu" + s, 0, CH)
+        mm([(pb, B("id"), B("xr_" + s, j * CH, (j + 1) * CH), j == 0, j == 7) for j in range(8)])
+        act(F("yp_" + s), pb, ACT.Identity)
+        store2("SY", T.yp, c, F("yp_" + s), 32768)
+        a = _F["yfo_" + s][0]
+        for h in range(2):
+            dma("Y", T.yf[4 * c:4 * c + 4, h * CH:(h + 1) * CH], T.FF[64 * h:64 * h + 64:16, a:a + CH], [], [F("yfo_" + s)], 2048)
+
+    rk[0] = -50; arrange(0)
+    rk[0] = RANK["a1"]; arrange(1)
+    rk[0] = RANK["l"]; lut()
+    for t in range(TS):
+        for c in range(2):
+            for f, k in ((index, "i"), (gathers, "g"), (choose, "c")):
+                rk[0] = 10 * t + 5 * c + RANK[k]; f(t, c)
+    for c in range(2):
+        rk[0] = 10 * (TS - 1) + 5 * c + RANK["w"] + RANK["f"]; finish(c)
+    return ops
+
+
+def depend(ops):
+    last = {}
+    for n, o in enumerate(ops):
+        deps = set()
+        for keys, w in ((o["rd"], False), (o["wr"], True)):
+            for name, lo, hi in keys:
+                for m, a, b, ww in last.get(name, []):
+                    if a < hi and lo < b and (w or ww): deps.add(m)
+        if o["par"]:
+            deps.discard(n - 1)
+        else:
+            for name, lo, hi in o["wr"]:
+                last[name] = [e for e in last.get(name, []) if not (lo <= e[1] and e[2] <= hi)]
+        for keys, w in ((o["rd"], False), (o["wr"], True)):
+            for e in set(keys):
+                last.setdefault(e[0], []).append((n, e[1], e[2], w))
+        deps.discard(n)
+        o["deps"] = sorted(deps)
+
+
+def order(ops):
+    n = len(ops)
+    users = [[] for o in ops]
+    for j, o in enumerate(ops):
+        for d in o["deps"]: users[d].append(j)
+    pri = [0.0] * n
+    for j in range(n - 1, -1, -1):
+        pri[j] = ops[j]["lat"] + max([pri[u] + WAKE for u in users[j]] + [0.0])
+    left = [len(o["deps"]) for o in ops]
+    rdy = [0.0] * n
+    free = {q: 0.0 for q in "VSPGY"}
+    cand = {q: [] for q in "VSPGY"}
+    for j, o in enumerate(ops):
+        if left[j] == 0: cand[o["q"]].append(j)
+    seq = []
+    while len(seq) < n:
+        best = None
+        for q in cand:
+            if cand[q]:
+                e = max(free[q], min(rdy[j] for j in cand[q]))
+                if best is None or e < best[0]: best = (e, q)
+        e, q = best
+        j = max((j for j in cand[q] if rdy[j] <= e + 50.0), key=lambda j: (-ops[j]["rank"], pri[j], -j))
+        cand[q].remove(j)
+        st = max(free[q], rdy[j]); free[q] = st + ops[j]["occ"]
+        ops[j]["start"] = st; seq.append(j)
+        for u in users[j]:
+            pp = ops[j]["q"] == "P" and ops[u]["q"] == "P"
+            rdy[u] = max(rdy[u], st + (ops[j]["occ"] if pp else ops[j]["lat"] + WAKE))
+            left[u] -= 1
+            if left[u] == 0: cand[ops[u]["q"]].append(u)
+    return seq
+
+
+def rank_program(g, core, T, topo):
+    if T.rank_of(core) is None:
+        return
+    ops = build(g, core, T, topo)
+    depend(ops)
+    seq = order(ops)
+    queue = {"V": g.vector, "S": g.scalar, "P": g.tensor, "G": g, "Y": g.sync}
+    csem = {"V": T.sem.cV, "S": T.sem.cS, "P": T.sem.cP, "G": T.sem.cG}
+    cnt = {q: 0 for q in csem}
+    seen = {q: {} for q in queue}
+    sent = 0
+    for j in seq:
+        o = ops[j]; q = o["q"]
+        need = {}
+        for d in o["deps"]:
+            p = ops[d]
+            if p["kind"] == "c":
+                if p["q"] == "P" and q == "P": continue
+                key, sem, val = p["q"], csem[p["q"]], p["num"]
+            else:
+                key, sem, val = d, p["sem"][0], p["sem"][1]
+            if val > need.get(key, (None, 0))[1]: need[key] = (sem, val)
+        for key, (sem, val) in need.items():
+            if seen[q].get(key, 0) < val:
+                queue[q].wait_ge(sem, val); seen[q][key] = val
+        r = o["fn"]()
+        if o["kind"] == "c":
+            cnt[q] += 1; o["num"] = cnt[q]; r.then_inc(csem[q], 1)
+        elif o["kind"] == "d":
+            r.then_inc(o["sem"][0], 16)
+        else:
+            sent += o["sem"][1]
+    for q in csem:
+        g.wait_ge(csem[q], cnt[q])
+    for o in ops:
+        if o["kind"] != "c": g.wait_ge(o["sem"][0], o["sem"][1])
+    g.wait_ge(T.sem.sent, sent)

@@ -11,11 +11,14 @@ WINW = 241 * 16
 M23 = 12582912.0
 M29 = 805306368.0
 XT = ["dddddddddddddd", "dddddddddddddd"]
-YT = ["ddddddddbbbbbb", "dddddddddbbbbb"]
-ON = {"nm": "VV", "z2": "SS", "zout": "SV", "t2": "VV", "rr": "VV", "zp": "VV", "na": "VV"}
-RANK = {"i": -7, "g": 1.5, "c": -6, "u": -10, "w": -6, "n": -4.0, "a1": -1, "l": 29, "G": 2, "f": 4, "d": 0.01}
+YT = ["ddddddddbbbbbb", "dddddddbbbbbbb"]
+ON = {"nm": "VV", "z2": "VV", "zout": "SS", "t2": "VV", "rr": "VV", "zp": "VV", "na": "VV"}
+RANK = {"i": -6.5, "g": -2.5, "c": -9.5, "u": -12.5, "w": -3.0, "n": -2.5, "a1": -3.0, "l": 23.5, "G": 0.5, "f": 12.0, "d": 0.01, "ap": -3.5}
 AB0 = 64.0 * 2880 - 13024
 SPLIT = True
+USCAN = False
+WPE = True
+ZR = 1
 GS, RG = 7, 7
 
 _F, _I, _B, _U = {}, {}, {}, {}
@@ -31,7 +34,7 @@ def _lay(tab, items):
 
 
 NF = _lay(_F, [("ix", 256), ("hi", 256), ("lo", 256), ("h16", 128), ("h64", 128), ("col", 16), ("yf32", 144), ("if32", 128), ("sw32", 128),
-               ("jj", 16), ("jt", 16), ("ctile", 8), ("e1", 256), ("e2", 256), ("qq_", 2048), ("bw_", 8), ("ye_", 8), ("cs_", 16), ("junk_", 8),
+               ("rs", 128), ("ctile", 8), ("e1", 256), ("e2", 256), ("un", 128), ("bw_", 8), ("ye_", 8), ("cs_", 16), ("junk_", 8),
                ("nm1_", 128), ("nm_", 128), ("na_", 224), ("n64_", 128), ("vk_", NP), ("ww_", NP), ("kk_", NP), ("t1_", 56), ("t2_", 32),
                ("t3_", 16), ("mx_", 8), ("mxe_", 8), ("aa_", 8), ("fl_", 8), ("cu_", 8), ("gg_", 224), ("mm_", 224), ("dl_", 224), ("d1_", NP),
                ("s1_", NP), ("id_", 128), ("sel_", 128), ("ta_", 128), ("wd_", 128), ("b1_", 128), ("b2_", 128), ("c2_", 128), ("q_", 128),
@@ -39,8 +42,8 @@ NF = _lay(_F, [("ix", 256), ("hi", 256), ("lo", 256), ("h16", 128), ("h64", 128)
 NI = _lay(_I, [("p", 2), ("k", 2), ("l8", 2), ("g48", 2), ("prod_", 224), ("sh_", 224), ("sm_", 224), ("base_", 224), ("m_", 8), ("cd_", 16),
                ("o2_", 8), ("ui_", 8), ("u15_", 8), ("ti_", 128), ("fd_", 128), ("th_", 8)])
 NB = _lay(_B, [("yn", 144), ("yp", 144), ("id", 128), ("nid", 128), ("i4", 128), ("i8", 128), ("i7", 128), ("bm", 128), ("bm2", 128),
-               ("sw", 128), ("tri", 128), ("trt", 128), ("b0", 128), ("b1", 128), ("cx", NP), ("cy", NP), ("ci", 128), ("m192", 256), ("p8", 2),
-               ("lut", 768), ("lt", 512), ("frac_", 128), ("sg_", 8), ("t2_", 128), ("s_", 128), ("zp_", 128), ("xo_", 128), ("rr_", 256),
+               ("sw", 128), ("dg", 128), ("up", 128), ("tri", 128), ("trt", 128), ("b0", 128), ("b1", 128), ("cx", NP), ("cy", NP), ("ci", 128), ("m192", 256), ("p8", 2),
+               ("lut", 768), ("lt", 512), ("frac_", 128), ("sg_", 8), ("t2_", 128), ("s_", 128), ("zp_", 128), ("xo_", 128), ("zr_", 512), ("rr_", 256),
                ("low_", 128), ("low8_", 128), ("free_", 128), ("ee_", 128), ("rw_", 128), ("xr_", 1792), ("ya_", 1792)])
 NU = _lay(_U, [("lbc", 8), ("lna", 14), ("lnb", 14), ("offs_", 224), ("o_", 16), ("c_", 16), ("fo_", 72)])
 
@@ -50,6 +53,7 @@ SCRATCH = {
     "nmi": ("sbuf", [128, 256], "int32"), "pri": ("sbuf", [128, 256], "int32"),
     "zin": ("sbuf", [128, 7 * 256], "bfloat16"), "zout": ("sbuf", [128, 6 * 256], "bfloat16"),
     "stin": ("sbuf", [128, 7 * 256], "float32"), "stout": ("sbuf", [128, 6 * 256], "float32"),
+    "HH": ("sbuf", [128, 8992], "float16"),
     "FF": ("sbuf", [128, NF], "float32"), "II": ("sbuf", [128, NI], "int32"),
     "BB": ("sbuf", [128, NB], "bfloat16"), "UU": ("sbuf", [128, NU], "uint16"),
 }
@@ -58,8 +62,9 @@ for _n in BANKS:
     SCRATCH[_n] = ("psum", [128, 512], "float32")
 SEMAPHORES = (["cV", "cS", "cP", "cG", "sent"] + ["ar%d" % i for i in range(4 * TS)] + ["dm%d" % i for i in range(40)])
 
-CYC, PCY, GR, SR = 1.0, 0.5, 1.56, 3.5
-WAKE, RLAT, DLAT, DISS = 60.0, 3000.0, 2000.0, 80.0
+CYC, PCY, GR, SR = 0.9, 0.5, 1.8, 3.5
+OVH = 40.0
+WAKE, RLAT, DLAT, DISS = 100.0, 4500.0, 2000.0, 80.0
 
 
 def build(g, core, T, topo):
@@ -71,7 +76,7 @@ def build(g, core, T, topo):
     def R(name, lo, hi, step=1):
         ap = T[name][:, lo:hi] if step == 1 else T[name][:, lo:hi:step]
         ps = name in BANKS
-        wide = name not in ("X0", "X1", "win0", "win1", "zin", "zout", "BB", "UU")
+        wide = name not in ("X0", "X1", "win0", "win1", "zin", "zout", "BB", "UU", "HH")
         return {"ap": ap, "keys": [(name, 0, 512)] if ps else [(name, lo, hi)], "n": len(range(lo, hi, step)), "ps": ps, "wide": wide, "ind": False}
 
     def sub(tab, buf):
@@ -87,6 +92,7 @@ def build(g, core, T, topo):
 
     def add(q, fn, outs, ins, occ, lat=None, kind="c", sem=None, par=False):
         rd, wr = [], []
+        if q in "VS" and kind == "c" and not any(isinstance(o, dict) and o["ind"] for o in outs + ins): occ += OVH
         for o in outs:
             if o["ind"]:
                 wr += o["wk"]; rd += o["ok"]
@@ -179,7 +185,7 @@ def build(g, core, T, topo):
         add("G", lambda: g.remote_dma(dst["ap"], src["ap"], sem, T.sem.sent, pid, rid, mask), [dst], [src], 150, RLAT, "r", (sem, ne))
 
     col = lambda j: F("col", j, j + 1)
-    PCOL, KCOL, G15, G16, L8, K16, LT8, GE8, P8, G48, P64, H2K = [col(j) for j in range(12)]
+    PCOL, KCOL, G15, G16, L8, K16, LT8, GE8, P8, G48, P64, H2K, K256 = [col(j) for j in range(13)]
     seln = lambda i: B("yn", 15 - i, 143 - i)
     selp = lambda i: B("yp", 15 - i, 143 - i)
     self32 = lambda i: F("yf32", 15 - i, 143 - i)
@@ -204,7 +210,7 @@ def build(g, core, T, topo):
     iota(I("p", 0, 1), [[0, 1]], 0, 1, False)
     iota(F("ix"), [[1, 256]], 0, 0)
     iota(F("h16"), [[16, 8], [0, 16]], 0, 0)
-    iota(B("ci"), [[240, 16], [0, 8]], 240, 0)
+    iota(B("ci"), [[1, 16], [0, 8]], 0, 0)
     ts(I("k", 0, 1), I("p", 0, 1), 15, None, ALU.bitwise_and)
     cp(PCOL, I("p", 0, 1)); cp(KCOL, I("k", 0, 1))
     tt(G16, PCOL, KCOL, ALU.subtract)
@@ -222,13 +228,18 @@ def build(g, core, T, topo):
     for name, v in (("i7", 458752.0), ("i4", -4096.0)):
         act(B(name), B("id"), ACT.Identity, scale=v)
     ts(F("yf32"), ix(0, 144), G15, None, ALU.is_equal)
+    ts(R("HH", 8704, 8848), F("yf32"), 16.0, None, ALU.mult)
+    ts(R("HH", 8848, 8992), F("yf32"), 1.0 / 16, None, ALU.mult)
+    act(K256, KCOL, ACT.Identity, bias=256.0)
+    act(B("up"), B("ci"), ACT.Exp, bias=16.0 * math.log(2.0), scale=-math.log(2.0))
+    act(F("un"), B("ci"), ACT.Identity, bias=-31.0 * 4112 - 1696.0 - 15.0 / 32, scale=4112.0)
     rk[0] = -40
+    act(F("if32"), B("id"), ACT.Identity)
     iota(F("h64"), [[0, 2], [16, 4], [0, 16]], 0, 0)
     iota(F("hi"), [[1, 16], [0, 16]], 0, 0)
     iota(F("lo"), [[0, 16], [1, 16]], 0, 0)
     for name, v in (("nid", -1.0), ("i8", -8192.0)):
         act(B(name), B("id"), ACT.Identity, scale=v)
-    act(F("if32"), B("id"), ACT.Identity)
     act(B("yn"), F("yf32"), ACT.Identity, scale=-2048.0)
     act(B("yp"), F("yf32"), ACT.Identity, scale=4096.0)
     ts(I("l8", 0, 1), I("p", 0, 1), 7, None, ALU.bitwise_and)
@@ -236,7 +247,10 @@ def build(g, core, T, topo):
     cp(L8, I("l8", 0, 1)); cp(G48, I("g48", 0, 1))
     ts(U("lbc"), ix(0, 8), 0.0, L8, ALU.mult, ALU.add)
     act(B("cx"), ix(0, NP), ACT.Identity, bias=float(CX))
-    act(B("cy"), ix(0, NP), ACT.Identity, bias=float(CY))
+    act(B("cy", 0, 56), ix(0, 56), ACT.Identity, bias=float(CX + CY + 56 - 128), scale=2.0)
+    act(B("cy", 56, NP), ix(56, NP), ACT.Identity, bias=float(CX + CY - 56 - 128), scale=2.0)
+    ts(B("dg"), F("lo", 0, CH), KCOL, -16384.0, ALU.not_equal, ALU.mult)
+    ts(F("rs"), F("lo", 0, CH), 0.0, None, ALU.is_gt)
     for c in range(2):
         ms(F("cs_%d" % c, 5, 6), AB0)
         ms(R("win%d" % c, 0, 272), 128.0)
@@ -249,7 +263,7 @@ def build(g, core, T, topo):
     ts(F("sw32"), ix(0, 128), -64.0, P64, ALU.add, ALU.is_equal)
     act(B("sw"), F("sw32"), ACT.Identity)
     for c in range(2):
-        ts(F("bw_%d" % c, 0, 6), I("th_%d" % c, 0, 6), -4096.0, -2176.0, ALU.mult, ALU.add)
+        ts(F("bw_%d" % c, 0, 6), I("th_%d" % c, 0, 6), -4096.0, -2048.0, ALU.mult, ALU.add)
     ms(B("m192"), -192.0)
 
     def arrange(c):
@@ -272,21 +286,29 @@ def build(g, core, T, topo):
         tt(F("wd_" + s), w0, F("ta_" + s), ALU.add)
         tt(I("ti_" + s), F("wd_" + s), B("ee_" + s), ALU.mult)
         ts(I("fd_" + s), I("ti_" + s), 3, 7, ALU.arith_shift_right, ALU.bitwise_and)
-        ts(F("b1_" + s), nm, 16.0, KCOL, ALU.mult, ALU.add)
-        ts(F("c2_" + s), pr, KCOL, 458752.0, ALU.is_le, ALU.mult)
+        ts(F("c2_" + s), pr, KCOL, 7.0, ALU.is_le, ALU.mult)
         tt(F("b2_" + s), pb, B("free_" + s), ALU.mult)
-        tt(F("b1_" + s), F("b1_" + s), F("c2_" + s), ALU.add)
-        tt(F("b2_" + s), F("b2_" + s), F("b1_" + s), ALU.add)
-        ts(F("q_" + s), I("fd_" + s), 65536.0, None, ALU.mult)
-        tt(F("q_" + s), F("q_" + s), F("b2_" + s), ALU.add)
-        mm([(R(po, 0, 128), B("i4"), B("ci"), True, False)])
-        for h in range(2):
-            for p in range(8 * h, 8 * h + 8):
-                ts(F("qq_" + s, p * CH, (p + 1) * CH), F("q_" + s), 65536.0 * p, 65536.0 * (p + 1), ALU.max, ALU.min)
-            for i0 in range(0, 16, 2):
-                mm([(R(po, 64 * h, 64 * h + 64), self32(i), F("qq_" + s, 1024 * h + i, 1024 * (h + 1), 16), False, h == 1 and i == 15)
-                    for i in range(i0, i0 + 2)])
-        act(stin(0, c), R(po, 0, 128), ACT.Identity, bias=-1696.0 - 15.0 / 32, scale=1.0 / 16)
+        ts(F("b2_" + s), F("b2_" + s), 1.0 / 65536, None, ALU.mult)
+        tt(F("b2_" + s), F("b2_" + s), F("c2_" + s), ALU.add)
+        ts(I("prod_" + s, 0, CH), nm, 4, None, ALU.arith_shift_right)
+        ts(I("sh_" + s, 0, CH), nm, 15, None, ALU.bitwise_and)
+        ts(F("b1_" + s), I("prod_" + s, 0, CH), 256.0, None, ALU.add)
+        ts(F("c2_" + s), I("sh_" + s, 0, CH), 16.0, K256, ALU.mult, ALU.add)
+        tt(F("q_" + s), I("fd_" + s), F("b2_" + s), ALU.add)
+        act(B("ee_" + s), F("q_" + s), ACT.Exp, bias=-16.0 * math.log(2.0), scale=math.log(2.0))
+        H = lambda a, b, st=1: R("HH", 4352 * c + a, 4352 * c + b, st)
+        tt(H(0, CH), F("b1_" + s), B("ee_" + s), ALU.mult)
+        tt(H(CH, 2 * CH), F("c2_" + s), B("ee_" + s), ALU.mult)
+        for y in range(2):
+            for p in range(16):
+                ts(H(256 + 2048 * y + p * CH, 256 + 2048 * y + (p + 1) * CH), H(y * CH, (y + 1) * CH), 2.0 ** (p - 8), 2.0 ** (p - 7), ALU.max, ALU.min)
+        if c == 1: rk[0] = RANK["ap"]
+        for y in range(2):
+            for i0 in range(0, 16, 4):
+                mm([(R(po, 0, CH), R("HH", 8704 + 144 * y + 15 - i, 8704 + 144 * y + 143 - i), H(256 + 2048 * y + i, 256 + 2048 * (y + 1), 16),
+                     y == 0 and i == 0, y == 1 and i == 15) for i in range(i0, i0 + 4)])
+        tt(F("q_" + s), R(po, 0, CH), B("up"), ALU.mult)
+        tt(stin(0, c), F("q_" + s), F("un"), ALU.add)
 
     def unpack(t, c, n):
         s = str(c)
@@ -347,6 +369,15 @@ def build(g, core, T, topo):
         xr = lambda a, b: B("xr_" + s, a * CH, b * CH)
         ya = lambda a, b, st=1, i=0: B("ya_" + s, a * CH + i, b * CH, st)
 
+        def gcopy(out, in0):
+            add("G", lambda: g.affine_select(A(out), A(in0), [[0, in0["n"]]], ALU.is_equal, 0.0, 0, 0), [out], [in0], 170 + 2 * in0["n"] * CYC)
+        for j in range(ZR if ZR > 1 else 0): gcopy(B("zr_" + s, j * CH, (j + 1) * CH), z)
+
+        def vblock(ty, a, b, dst):
+            for j in range(a, b, ZR):
+                e = min(b, j + ZR)
+                tt(dst(j, e), ind(Xw, off(ty, j, e)), z if e == j + 1 else B("zr_" + s, 0, (e - j) * CH), ALU.subtract)
+
         def dblock(ty, a, b, raw, dst):
             rk[0] += RANK["d"]
             act(raw(a, b), ind(Xw, off(ty, a, b)), ACT.Copy)
@@ -358,34 +389,36 @@ def build(g, core, T, topo):
                 act(dst(a1, b1), R(pb, 0, (b1 - a1) * CH), ACT.Abs, scale=2.0)
         mm([(R("pd", 0, NP), B("id"), B("cx"), True, False), (R("pd", 0, NP), B("i4"), B("frac_" + s, 0, NP), False, False)])
         mm([(R(pu, 0, NP), B("id"), B("cy"), True, False),
-            (R(pu, 0, 56), B("id"), B("cx", 56, NP), False, False), (R(pu, 56, NP), B("id"), B("cx", 0, 56), False, False),
             (R(pu, 0, 56), B("i8"), B("frac_" + s, 56, NP), False, False), (R(pu, 56, NP), B("i8"), B("frac_" + s, 0, 56), False, False)])
         for lo in range(0, 14, RG):
             hi = lo + RG
             for a, b in runs(xt, "d", GS, lo, hi): dblock(0, a, b, xr, wx)
             for a, b in runs(xt, "b", 7, lo, hi):
-                for j in range(a, b): tt(xr(j, j + 1), ind(Xw, off(0, j, j + 1)), z, ALU.subtract)
+                vblock(0, a, b, xr)
                 act(wx(a, b), xr(a, b), ACT.Abs, scale=2.0)
             mm([(R("pd", 8 * lo, 8 * hi), seln(i), wx(lo, hi, 16, i), False, hi == 14 and i == 15) for i in range(16)])
-        act(F("ww_" + s), R("pd", 0, NP), ACT.Identity, bias=F("bw_" + s, t, t + 1), scale=-1.0)
+        if WPE:
+            act(F("ww_" + s), R("pd", 0, NP), ACT.Identity, bias=F("bw_" + s, t, t + 1), scale=-1.0)
+            mm([(R(pu, 0, 56), F("if32"), F("ww_" + s, 56, NP), False, False), (R(pu, 56, NP), F("if32"), F("ww_" + s, 0, 56), False, False)])
+        for h in range(0 if WPE else 2):
+            act(F("ww_" + s, 56 * h, 56 * h + 56), R("pd", 56 - 56 * h, NP - 56 * h), ACT.Identity, bias=F("bw_" + s, t, t + 1), scale=-1.0)
         act(F("vk_" + s), R("pd", 0, NP), ACT.Identity, bias=4130688.0 / 16777216.0, scale=1.0 / 16777216.0)
         for lo in range(0, 14, RG):
             hi = lo + RG
             for a, b in runs(yt, "d", GS, lo, hi): dblock(1, a, b, wy, ya)
             for a, b in runs(yt, "ab", 7, lo, hi):
-                for j in range(a, b): tt(wy(j, j + 1), ind(Xw, off(1, j, j + 1)), z, ALU.subtract)
+                vblock(1, a, b, wy)
                 if yt[a] == "a": ts(ya(a, b), wy(a, b), 0.0, 4.0, ALU.max, ALU.mult)
                 else: act(ya(a, b), wy(a, b), ACT.Abs, scale=2.0)
             for a, b in runs(yt, "a", 14, lo, hi):
                 mm([(R(pu, 8 * a, 8 * b), selp(i), wy(a, b, 16, i), False, False) for i in range(16)])
-            if hi == 14:
-                mm([(R(pu, 0, 56), F("if32"), F("ww_" + s, 56, NP), False, False), (R(pu, 56, NP), F("if32"), F("ww_" + s, 0, 56), False, False)])
             mm([(R(pu, 8 * lo, 8 * hi), seln(i), ya(lo, hi, 16, i), False, hi == 14 and i == 15) for i in range(16)])
 
     def choose(t, c):
         s = str(c); wn = "win" + s
         K = lambda a=0, b=NP: F("kk_" + s, a, b)
         mx = F("mx_" + s)
+        if not WPE: tt(R("pu" + s, 0, NP), R("pu" + s, 0, NP), F("ww_" + s), ALU.add)
         tt(K(), R("pu" + s, 0, NP), F("vk_" + s), ALU.max)
         tt(F("t1_" + s), K(0, 56), K(56, NP), ALU.max)
         tt(F("t2_" + s), F("t1_" + s, 0, 32), F("t1_" + s, 24, 56), ALU.max)
@@ -416,8 +449,15 @@ def build(g, core, T, topo):
         lin(ON["zout"][c], zout(t, c), B("zp_" + s), 1.0, -128.0)
         send(zin(t + 1, c), zout(t, c), rank + 1 if t < TS - 1 else rank - (TS - 1))
         rk[0] = 10 * t + 5 * c + RANK["w"]
-        mm([(R("pz", 0, 8), selp(i), B("zp_" + s, i, CH, 16), i == 0, i == 15) for i in range(16)])
-        ts(I("ui_" + s), R("pz", 0, 8), 1.0 / 4096, None, ALU.mult)
+        if USCAN:
+            pq = R("pz", 256, 384)
+            mm([(pq, B("id"), B("dg"), True, False), (pq, B("bm"), B("zp_" + s), False, True)])
+            add("V", lambda: g.vector.tensor_tensor_scan(A(F("ta_" + s)), A(F("rs")), A(pq), 0.0, ALU.mult, ALU.max),
+                [F("ta_" + s)], [F("rs"), pq], CH * CYC)
+            cp(I("ui_" + s), F("ta_" + s, 15, CH, 16))
+        else:
+            mm([(R("pz", 0, 8), selp(i), B("zp_" + s, i, CH, 16), i == 0, i == 15) for i in range(16)])
+            ts(I("ui_" + s), R("pz", 0, 8), 1.0 / 4096, None, ALU.mult)
         ts(I("u15_" + s), I("ui_" + s), 15, None, ALU.bitwise_and)
         tt(F("cu_" + s), I("u15_" + s), F("ctile"), ALU.add)
         cp(U("c_" + s, 0, 8), F("cu_" + s))
@@ -449,8 +489,8 @@ def build(g, core, T, topo):
         tt(d1(0, 16), d1(0, 16), d1(16, 32), ALU.add)
         tt(stout(t, c, 112, 120), stin(t, c, 112, 120), d1(0, 16, 2), ALU.subtract)
         tt(stout(t, c, 120, 128), stin(t, c, 120, 128), d1(1, 16, 2), ALU.subtract)
-        tt(F("s1_" + s), stin(t, c, 0, NP), dl(0, 224, 2), ALU.add)
-        tt(stout(t, c, 0, NP), F("s1_" + s), dl(1, 224, 2), ALU.add)
+        tt(F("mm_" + s, NP, 224), stin(t, c, 0, NP), dl(0, 224, 2), ALU.add)
+        tt(stout(t, c, 0, NP), F("mm_" + s, NP, 224), dl(1, 224, 2), ALU.add)
         send(stin(t + 1, c), stout(t, c), rank + 1 if t < TS - 1 else rank - (TS - 1))
 
     def count(t, c):

import math
from concourse.mybir import AluOpType, ActivationFunctionType

ALU = AluOpType
ACT = ActivationFunctionType
TS, NR = 6, 4
CH = 128
NP = 112
CX, CY = 17, 129
WINW = 241 * 16
M23 = 12582912.0
M29 = 805306368.0
XT = ["dddddddddddddd", "dddddddddddddd"]
YT = ["ddddddddbbbbbb", "dddddddbbbbbbb"]
ON = {"nm": "VV", "z2": "VV", "zout": "SS", "t2": "VV", "rr": "VV", "zp": "VV", "na": "VV"}
RANK = {"i": -6.5, "g": -2.5, "c": -9.5, "u": -12.5, "w": -3.0, "n": -2.5, "a1": -3.0, "l": 23.5, "G": 0.5, "f": 12.0, "d": 0.01, "ap": -3.5}
AB0 = 64.0 * 2880 - 13024
SPLIT = True
USCAN = False
WPE = True
ZR = 1
GS, RG = 7, 7

_F, _I, _B, _U = {}, {}, {}, {}


def _lay(tab, items):
    n = 0
    for name, w in items:
        for c in (range(2) if name.endswith("_") else [None]):
            tab[name if c is None else name + str(c)] = (n, w)
            n += (w + 15) // 16 * 16
    return n


NF = _lay(_F, [("ix", 256), ("hi", 256), ("lo", 256), ("h16", 128), ("h64", 128), ("col", 16), ("yf32", 144), ("if32", 128), ("sw32", 128),
               ("rs", 128), ("ctile", 8), ("e1", 256), ("e2", 256), ("un", 128), ("bw_", 8), ("ye_", 8), ("cs_", 16), ("junk_", 8),
               ("nm1_", 128), ("nm_", 128), ("na_", 224), ("n64_", 128), ("vk_", NP), ("ww_", NP), ("kk_", NP), ("t1_", 56), ("t2_", 32),
               ("t3_", 16), ("mx_", 8), ("mxe_", 8), ("aa_", 8), ("fl_", 8), ("cu_", 8), ("gg_", 224), ("mm_", 224), ("dl_", 224), ("d1_", NP),
               ("s1_", NP), ("id_", 128), ("sel_", 128), ("ta_", 128), ("wd_", 128), ("b1_", 128), ("b2_", 128), ("c2_", 128), ("q_", 128),
               ("f16_", 128), ("pc_", 64), ("yp_", 128), ("yfo_", 128)])
NI = _lay(_I, [("p", 2), ("k", 2), ("l8", 2), ("g48", 2), ("prod_", 224), ("sh_", 224), ("sm_", 224), ("base_", 224), ("m_", 8), ("cd_", 16),
               ("o2_", 8), ("ui_", 8), ("u15_", 8), ("ti_", 128), ("fd_", 128), ("th_", 8)])
NB = _lay(_B, [("yn", 144), ("yp", 144), ("id", 128), ("nid", 128), ("i4", 128), ("i8", 128), ("i7", 128), ("bm", 128), ("bm2", 128),
               ("sw", 128), ("dg", 128), ("up", 128), ("tri", 128), ("trt", 128), ("b0", 128), ("b1", 128), ("cx", NP), ("cy", NP), ("ci", 128), ("m192", 256), ("p8", 2),
               ("lut", 768), ("lt", 512), ("frac_", 128), ("sg_", 8), ("t2_", 128), ("s_", 128), ("zp_", 128), ("xo_", 128), ("zr_", 512), ("rr_", 256),
               ("low_", 128), ("low8_", 128), ("free_", 128), ("ee_", 128), ("rw_", 128), ("xr_", 1792), ("ya_", 1792)])
NU = _lay(_U, [("lbc", 8), ("lna", 14), ("lnb", 14), ("offs_", 224), ("o_", 16), ("c_", 16), ("fo_", 72)])

SCRATCH = {
    "X0": ("sbuf", [128, 4096], "bfloat16"), "X1": ("sbuf", [128, 4096], "bfloat16"),
    "win0": ("sbuf", [128, WINW], "bfloat16"), "win1": ("sbuf", [128, WINW], "bfloat16"),
    "nmi": ("sbuf", [128, 256], "int32"), "pri": ("sbuf", [128, 256], "int32"),
    "zin": ("sbuf", [128, 7 * 256], "bfloat16"), "zout": ("sbuf", [128, 6 * 256], "bfloat16"),
    "stin": ("sbuf", [128, 7 * 256], "float32"), "stout": ("sbuf", [128, 6 * 256], "float32"),
    "HH": ("sbuf", [128, 8992], "float16"),
    "FF": ("sbuf", [128, NF], "float32"), "II": ("sbuf", [128, NI], "int32"),
    "BB": ("sbuf", [128, NB], "bfloat16"), "UU": ("sbuf", [128, NU], "uint16"),
}
BANKS = ("ps0", "ps1", "ps2", "pi", "pd", "pu0", "pu1", "pz")
for _n in BANKS:
    SCRATCH[_n] = ("psum", [128, 512], "float32")
SEMAPHORES = (["cV", "cS", "cP", "cG", "sent"] + ["ar%d" % i for i in range(4 * TS)] + ["dm%d" % i for i in range(40)])

CYC, PCY, GR, SR = 0.9, 0.5, 1.8, 3.5
OVH = 40.0
WAKE, RLAT, DLAT, DISS = 100.0, 4500.0, 2000.0, 80.0


def build(g, core, T, topo):
    rank = T.rank_of(core)
    ops = []
    rk = [-100]
    bank = [0]

    def R(name, lo, hi, step=1):
        ap = T[name][:, lo:hi] if step == 1 else T[name][:, lo:hi:step]
        ps = name in BANKS
        wide = name not in ("X0", "X1", "win0", "win1", "zin", "zout", "BB", "UU", "HH")
        return {"ap": ap, "keys": [(name, 0, 512)] if ps else [(name, lo, hi)], "n": len(range(lo, hi, step)), "ps": ps, "wide": wide, "ind": False}

    def sub(tab, buf):
        def f(name, lo=0, hi=None, step=1):
            a, w = tab[name]
            return R(buf, a + lo, a + (w if hi is None else hi), step)
        return f
    F, I, B, U = sub(_F, "FF"), sub(_I, "II"), sub(_B, "BB"), sub(_U, "UU")

    def ind(win, off):
        return {"ap": win["ap"].indirect(off["ap"]), "keys": win["keys"] + off["keys"], "wk": win["keys"], "ok": off["keys"],
                "n": off["n"] * 16, "ps": False, "wide": True, "ind": True}

    def add(q, fn, outs, ins, occ, lat=None, kind="c", sem=None, par=False):
        rd, wr = [], []
        if q in "VS" and kind == "c" and not any(isinstance(o, dict) and o["ind"] for o in outs + ins): occ += OVH
        for o in outs:
            if o["ind"]:
                wr += o["wk"]; rd += o["ok"]
            else:
                wr += o["keys"]
        for o in ins:
            if isinstance(o, dict):
                if o["ps"]: wr += o["keys"]
                else: rd += o["keys"]
        ops.append({"q": q, "fn": fn, "rd": rd, "wr": wr, "occ": occ, "lat": occ if lat is None else lat, "kind": kind, "sem": sem,
                    "rank": rk[0], "par": par})

    A = lambda o: o["ap"] if isinstance(o, dict) else o

    def vcost(out, in0, rate):
        if out["ind"]: return 50 + SR * out["n"] * CYC
        if in0["ind"]: return 50 + GR * in0["n"] * CYC
        return max(64, rate * out["n"]) * CYC

    def ts(out, in0, s1, s2, op0, op1=None):
        rate = 1.0 if (out["wide"] or in0["wide"]) else 0.5
        if op1 is None: fn = lambda: g.vector.tensor_scalar(A(out), A(in0), A(s1), None, op0)
        else: fn = lambda: g.vector.tensor_scalar(A(out), A(in0), A(s1), A(s2), op0, op1)
        add("V", fn, [out], [in0, s1, s2], vcost(out, in0, rate))

    def tt(out, in0, in1, op):
        rate = 1.0 if (in0["ps"] or in1["ps"]) else 2.0
        add("V", lambda: g.vector.tensor_tensor(A(out), A(in0), A(in1), op), [out], [in0, in1], vcost(out, in0, rate))

    def cp(out, in0):
        rate = 1.0 if (out["wide"] or in0["wide"]) else 0.5
        add("V", lambda: g.vector.tensor_copy(A(out), A(in0)), [out], [in0], vcost(out, in0, rate))

    def ms(out, v):
        add("V", lambda: g.vector.memset(A(out), v), [out], [], max(64, out["n"] * 0.5) * CYC)

    def act(out, in0, func, bias=0.0, scale=1.0, acc=None):
        c = 65 + GR * in0["n"] * CYC if in0["ind"] else max(64, in0["n"]) * CYC
        if acc is None: fn = lambda: g.scalar.activation(A(out), A(in0), func, bias=A(bias), scale=A(scale))
        else: fn = lambda: g.scalar.activation(A(out), A(in0), func, bias=A(bias), scale=A(scale), accum_out=A(acc))
        add("S", fn, [out] + ([acc] if acc else []), [in0, bias, scale], c + (20 if acc else 0))

    def lin(e, out, in0, scale, bias):
        if e == "S": act(out, in0, ACT.Identity, bias=bias, scale=scale)
        else: ts(out, in0, scale, bias, ALU.mult, ALU.add)

    def mm(items):
        def fn():
            r = None
            for o, l, x, st, sp in items:
                r = g.tensor.matmul(o["ap"], l["ap"], x["ap"], st, sp)
            return r
        c = sum(max(64, x["n"]) * (4 if x["wide"] else 1) * PCY for o, l, x, st, sp in items)
        add("P", fn, [it[0] for it in items], [it[1] for it in items] + [it[2] for it in items], c, c + 60)

    def iota(out, pat, base, cm, flt=True):
        if flt: fn = lambda: g.iota(A(out), pat, base, cm, allow_small_or_imprecise_dtypes=True)
        else: fn = lambda: g.iota(A(out), pat, base, cm)
        add("G", fn, [out], [], 130 + 2 * out["n"] * CYC)

    nd = [0]

    def dma(q, out, in0, outs, ins, nbytes, par=False):
        sem = T.sem["dm%d" % nd[0]]; nd[0] += 1
        e = g.sync if q == "Y" else g.scalar
        add(q, lambda: e.dma_start(out, in0), outs, ins, DISS, DLAT + nbytes / 150.0, "d", (sem, 16), par)

    def halves(reg):
        name, lo, hi = reg["keys"][0]
        return T[name][0:64, lo:hi], T[name][64:128, lo:hi]

    def load2(qs, reg, src0, src1, nbytes):
        a, b = halves(reg)
        dma(qs[0], a, src0, [reg], [], nbytes)
        dma(qs[1], b, src1, [reg], [], nbytes, True)

    def store2(qs, dst, c, reg, nbytes):
        a, b = halves(reg)
        dma(qs[0], dst[64 * c:64 * c + 64, 0:CH], a, [], [reg], nbytes)
        dma(qs[1], dst[64 * c:64 * c + 64, CH:2 * CH], b, [], [reg], nbytes)

    na = [0]

    def send(dst, src, to):
        sem = T.sem["ar%d" % na[0]]; na[0] += 1
        peer = T.cores[to % NR]
        rid, pid, se = topo.addr(peer)
        mask = topo.mask(core, peer)
        ne = len(topo.engines(core, peer))
        add("G", lambda: g.remote_dma(dst["ap"], src["ap"], sem, T.sem.sent, pid, rid, mask), [dst], [src], 150, RLAT, "r", (sem, ne))

    col = lambda j: F("col", j, j + 1)
    PCOL, KCOL, G15, G16, L8, K16, LT8, GE8, P8, G48, P64, H2K, K256 = [col(j) for j in range(13)]
    seln = lambda i: B("yn", 15 - i, 143 - i)
    selp = lambda i: B("yp", 15 - i, 143 - i)
    self32 = lambda i: F("yf32", 15 - i, 143 - i)
    zin = lambda t, c: R("zin", (2 * t + c) * CH, (2 * t + c + 1) * CH)
    zout = lambda t, c: R("zout", (2 * t + c) * CH, (2 * t + c + 1) * CH)
    stin = lambda t, c, lo=0, hi=CH: R("stin", (2 * t + c) * CH + lo, (2 * t + c) * CH + hi)
    stout = lambda t, c, lo=0, hi=CH: R("stout", (2 * t + c) * CH + lo, (2 * t + c) * CH + hi)
    ix = lambda lo, hi: F("ix", lo, hi)
    XW = lambda c: R("X%d" % c, 0, 4096)
    cs = lambda c, j: F("cs_%d" % c, j, j + 1)

    for c in range(2):
        rk[0] = -100 + c
        rows = slice(64 * c, 64 * c + 64); qs = "YS" if c == 0 else "YY"
        load2(qs, R("pri", c * CH, (c + 1) * CH), T.pr[rows, 0:CH], T.pr[rows, CH:2 * CH], 32768)
        load2(qs, R("nmi", c * CH, (c + 1) * CH), T.nm[rows, 0:CH], T.nm[rows, CH:2 * CH], 32768)
        load2(qs, XW(c), T.xt[rows, :], T.xt[rows, :], 1048576 * (c + 1))
        load2("YY", zin(0, c), T.z0[rows, 0:CH], T.z0[rows, CH:2 * CH], 16384)
        load2("YY", I("th_%d" % c, 0, 6), T.th[rows, :], T.th[rows, :], 1536)

    rk[0] = -100
    iota(I("p", 0, 1), [[0, 1]], 0, 1, False)
    iota(F("ix"), [[1, 256]], 0, 0)
    iota(F("h16"), [[16, 8], [0, 16]], 0, 0)
    iota(B("ci"), [[1, 16], [0, 8]], 0, 0)
    ts(I("k", 0, 1), I("p", 0, 1), 15, None, ALU.bitwise_and)
    cp(PCOL, I("p", 0, 1)); cp(KCOL, I("k", 0, 1))
    tt(G16, PCOL, KCOL, ALU.subtract)
    ts(G15, G16, 15.0, None, ALU.add)
    ts(LT8, KCOL, 8.0, None, ALU.is_lt)
    ts(GE8, KCOL, 8.0, None, ALU.is_ge)
    act(B("p8", 0, 1), KCOL, ACT.Exp, bias=-16.0 * math.log(2.0), scale=math.log(8.0))
    act(P8, B("p8", 0, 1), ACT.Identity)
    ts(B("bm"), F("h16"), G16, None, ALU.is_equal)
    ts(B("trt"), ix(0, 128), PCOL, 65536.0, ALU.is_gt, ALU.mult)
    tt(B("tri"), B("trt"), B("bm"), ALU.mult)
    ts(B("b0"), B("bm"), LT8, None, ALU.mult)
    ts(B("b1"), B("bm"), GE8, None, ALU.mult)
    ts(B("id"), ix(0, 128), PCOL, None, ALU.is_equal)
    for name, v in (("i7", 458752.0), ("i4", -4096.0)):
        act(B(name), B("id"), ACT.Identity, scale=v)
    ts(F("yf32"), ix(0, 144), G15, None, ALU.is_equal)
    ts(R("HH", 8704, 8848), F("yf32"), 16.0, None, ALU.mult)
    ts(R("HH", 8848, 8992), F("yf32"), 1.0 / 16, None, ALU.mult)
    act(K256, KCOL, ACT.Identity, bias=256.0)
    act(B("up"), B("ci"), ACT.Exp, bias=16.0 * math.log(2.0), scale=-math.log(2.0))
    act(F("un"), B("ci"), ACT.Identity, bias=-31.0 * 4112 - 1696.0 - 15.0 / 32, scale=4112.0)
    rk[0] = -40
    act(F("if32"), B("id"), ACT.Identity)
    iota(F("h64"), [[0, 2], [16, 4], [0, 16]], 0, 0)
    iota(F("hi"), [[1, 16], [0, 16]], 0, 0)
    iota(F("lo"), [[0, 16], [1, 16]], 0, 0)
    for name, v in (("nid", -1.0), ("i8", -8192.0)):
        act(B(name), B("id"), ACT.Identity, scale=v)
    act(B("yn"), F("yf32"), ACT.Identity, scale=-2048.0)
    act(B("yp"), F("yf32"), ACT.Identity, scale=4096.0)
    ts(I("l8", 0, 1), I("p", 0, 1), 7, None, ALU.bitwise_and)
    ts(I("g48", 0, 1), I("p", 0, 1), 48, None, ALU.bitwise_and)
    cp(L8, I("l8", 0, 1)); cp(G48, I("g48", 0, 1))
    ts(U("lbc"), ix(0, 8), 0.0, L8, ALU.mult, ALU.add)
    act(B("cx"), ix(0, NP), ACT.Identity, bias=float(CX))
    act(B("cy", 0, 56), ix(0, 56), ACT.Identity, bias=float(CX + CY + 56 - 128), scale=2.0)
    act(B("cy", 56, NP), ix(56, NP), ACT.Identity, bias=float(CX + CY - 56 - 128), scale=2.0)
    ts(B("dg"), F("lo", 0, CH), KCOL, -16384.0, ALU.not_equal, ALU.mult)
    ts(F("rs"), F("lo", 0, CH), 0.0, None, ALU.is_gt)
    for c in range(2):
        ms(F("cs_%d" % c, 5, 6), AB0)
        ms(R("win%d" % c, 0, 272), 128.0)
    rk[0] = -1
    ts(H2K, PCOL, 64.0, 2048.0, ALU.is_ge, ALU.mult)
    act(K16, KCOL, ACT.Identity, bias=H2K, scale=16.0)
    ts(F("ctile"), ix(0, 8), 256.0, K16, ALU.mult, ALU.add)
    ts(B("bm2"), F("h64"), G48, None, ALU.is_equal)
    act(P64, H2K, ACT.Identity, bias=PCOL, scale=-1.0 / 16)
    ts(F("sw32"), ix(0, 128), -64.0, P64, ALU.add, ALU.is_equal)
    act(B("sw"), F("sw32"), ACT.Identity)
    for c in range(2):
        ts(F("bw_%d" % c, 0, 6), I("th_%d" % c, 0, 6), -4096.0, -2048.0, ALU.mult, ALU.add)
    ms(B("m192"), -192.0)

    def arrange(c):
        s = str(c)
        pr = R("pri", c * CH, (c + 1) * CH); nm = R("nmi", c * CH, (c + 1) * CH)
        if c == 0: pa, pb, w0, w1, po = R("ps0", 0, 128), R("ps1", 0, 128), R("ps2", 0, 128), R("pd", 0, 128), "pu0"
        else: pa, pb, w0, w1, po = R("pz", 0, 128), R("pu1", 128, 256), R("pz", 128, 256), R("pz", 256, 384), "pu1"
        ts(B("low_" + s), pr, KCOL, None, ALU.is_gt)
        ts(B("low8_" + s), pr, KCOL, P8, ALU.is_gt, ALU.mult)
        ts(B("free_" + s), pr, KCOL, None, ALU.is_equal)
        ts(F("id_" + s), pr, KCOL, None, ALU.min)
        mm([(pa, B("tri"), B("low_" + s), True, True)])
        tt(B("rw_" + s), pa, B("low8_" + s), ALU.mult)
        mm([(pb, B("tri"), B("free_" + s), True, False), (pb, B("i7"), B("free_" + s), False, True)])
        ts(F("sel_" + s), F("id_" + s), 8.0, None, ALU.is_ge)
        act(B("ee_" + s), F("id_" + s), ACT.Exp, bias=math.log(8.0), scale=-math.log(8.0))
        mm([(w1, B("b1"), B("rw_" + s), True, True)])
        mm([(w0, B("b0"), B("rw_" + s), True, True)])
        tt(F("ta_" + s), w1, F("sel_" + s), ALU.mult)
        tt(F("wd_" + s), w0, F("ta_" + s), ALU.add)
        tt(I("ti_" + s), F("wd_" + s), B("ee_" + s), ALU.mult)
        ts(I("fd_" + s), I("ti_" + s), 3, 7, ALU.arith_shift_right, ALU.bitwise_and)
        ts(F("c2_" + s), pr, KCOL, 7.0, ALU.is_le, ALU.mult)
        tt(F("b2_" + s), pb, B("free_" + s), ALU.mult)
        ts(F("b2_" + s), F("b2_" + s), 1.0 / 65536, None, ALU.mult)
        tt(F("b2_" + s), F("b2_" + s), F("c2_" + s), ALU.add)
        ts(I("prod_" + s, 0, CH), nm, 4, None, ALU.arith_shift_right)
        ts(I("sh_" + s, 0, CH), nm, 15, None, ALU.bitwise_and)
        ts(F("b1_" + s), I("prod_" + s, 0, CH), 256.0, None, ALU.add)
        ts(F("c2_" + s), I("sh_" + s, 0, CH), 16.0, K256, ALU.mult, ALU.add)
        tt(F("q_" + s), I("fd_" + s), F("b2_" + s), ALU.add)
        act(B("ee_" + s), F("q_" + s), ACT.Exp, bias=-16.0 * math.log(2.0), scale=math.log(2.0))
        H = lambda a, b, st=1: R("HH", 4352 * c + a, 4352 * c + b, st)
        tt(H(0, CH), F("b1_" + s), B("ee_" + s), ALU.mult)
        tt(H(CH, 2 * CH), F("c2_" + s), B("ee_" + s), ALU.mult)
        for y in range(2):
            for p in range(16):
                ts(H(256 + 2048 * y + p * CH, 256 + 2048 * y + (p + 1) * CH), H(y * CH, (y + 1) * CH), 2.0 ** (p - 8), 2.0 ** (p - 7), ALU.max, ALU.min)
        if c == 1: rk[0] = RANK["ap"]
        for y in range(2):
            for i0 in range(0, 16, 4):
                mm([(R(po, 0, CH), R("HH", 8704 + 144 * y + 15 - i, 8704 + 144 * y + 143 - i), H(256 + 2048 * y + i, 256 + 2048 * (y + 1), 16),
                     y == 0 and i == 0, y == 1 and i == 15) for i in range(i0, i0 + 4)])
        tt(F("q_" + s), R(po, 0, CH), B("up"), ALU.mult)
        tt(stin(0, c), F("q_" + s), F("un"), ALU.add)

    def unpack(t, c, n):
        s = str(c)
        if ON["nm"][c] == "S":
            act(F("nm1_" + s), stin(t, c), ACT.Identity, bias=M23)
            act(F("nm_" + s), F("nm1_" + s), ACT.Identity, bias=-M23)
        else:
            ts(F("nm_" + s), stin(t, c), M23, -M23, ALU.add, ALU.add)
        tt(B("frac_" + s, 0, n), stin(t, c, 0, n), F("nm_" + s, 0, n), ALU.subtract)

    def index(t, c):
        s = str(c); wn = "win" + s
        unpack(t, c, NP)
        nm = lambda a, b: F("nm_" + s, a, b)
        for h in range(2):
            act(R("pi", 56 * h, 56 * h + 56), nm(56 - 56 * h, NP - 56 * h), ACT.Identity, bias=2880.0)
        tt(I("prod_" + s, 0, NP), R("pi", 0, NP), nm(0, NP), ALU.mult)
        if ON["na"][c] == "S":
            act(F("na_" + s, 0, NP), ind(nm(112, 120), U("lbc", 0, 7)), ACT.Copy)
            tt(I("prod_" + s, NP, 224), R("pi", 0, NP), F("na_" + s, 0, NP), ALU.mult)
        else:
            for h in range(2):
                act(F("na_" + s, 56 * h, 56 * h + 56), nm(56 - 56 * h, NP - 56 * h), ACT.Identity, bias=2880.0)
            tt(I("prod_" + s, NP, 224), ind(nm(112, 120), U("lbc", 0, 7)), F("na_" + s, 0, NP), ALU.mult)
        for h in range(2):
            act(R("pi", 128 + 56 * h, 184 + 56 * h), nm(56 - 56 * h, NP - 56 * h), ACT.Identity, bias=cs(c, 5), scale=64.0)
        parts = ((0, NP), (NP, 224)) if SPLIT else ((0, 224),)
        for a, b in parts:
            ts(I("sh_" + s, a, b), I("prod_" + s, a, b), 5, None, ALU.arith_shift_right)
            for a1 in range(a, b, NP):
                tt(I("sm_" + s, a1, a1 + NP), R("pi", 128, 128 + NP), I("sh_" + s, a1, a1 + NP), ALU.add)
            ts(I("base_" + s, a, b), I("sm_" + s, a, b), 4095, None, ALU.bitwise_and)
            cp(U("offs_" + s, a, b), I("base_" + s, a, b))
        rk[0] = 10 * t + 5 * c + RANK["G"]
        tt(F("gg_" + s, 0, 224, 2), ind(stin(t, c, 112, 120), U("lbc", 0, 7)), stin(t, c, 0, NP), ALU.subtract)
        tt(F("gg_" + s, 1, 224, 2), ind(stin(t, c, 120, 128), U("lbc", 0, 7)), stin(t, c, 0, NP), ALU.subtract)
        if YT[c].count("d") < 14: lin(ON["z2"][c], R(wn, 16, 144), zin(t, c), 2.0, 128.0)
        if "d" in YT[c]: lin(ON["z2"][c], R(wn, 144, 272), zin(t, c), 1.0, 128.0)

    def runs(types, ch, most, lo, hi):
        out, j = [], lo
        while j < hi:
            if types[j] in ch:
                e = j
                while e < hi and types[e] == types[j] and e - j < most: e += 1
                out.append((j, e)); j = e
            else:
                j += 1
        return out

    def gathers(t, c):
        s = str(c); wn = "win" + s; pu = "pu" + s
        xt, yt = XT[c], YT[c]
        Xw = XW(c); z = zin(t, c)
        off = lambda ty, a, b: U("offs_" + s, ty * NP + 8 * a, ty * NP + 8 * b)
        wx = lambda a, b, st=1, i=0: R(wn, CX * 16 + a * CH + i, CX * 16 + b * CH, st)
        wy = lambda a, b, st=1, i=0: R(wn, CY * 16 + a * CH + i, CY * 16 + b * CH, st)
        xr = lambda a, b: B("xr_" + s, a * CH, b * CH)
        ya = lambda a, b, st=1, i=0: B("ya_" + s, a * CH + i, b * CH, st)

        def gcopy(out, in0):
            add("G", lambda: g.affine_select(A(out), A(in0), [[0, in0["n"]]], ALU.is_equal, 0.0, 0, 0), [out], [in0], 170 + 2 * in0["n"] * CYC)
        for j in range(ZR if ZR > 1 else 0): gcopy(B("zr_" + s, j * CH, (j + 1) * CH), z)

        def vblock(ty, a, b, dst):
            for j in range(a, b, ZR):
                e = min(b, j + ZR)
                tt(dst(j, e), ind(Xw, off(ty, j, e)), z if e == j + 1 else B("zr_" + s, 0, (e - j) * CH), ALU.subtract)

        def dblock(ty, a, b, raw, dst):
            rk[0] += RANK["d"]
            act(raw(a, b), ind(Xw, off(ty, a, b)), ACT.Copy)
            for a1 in range(a, b, 4):
                b1 = min(b, a1 + 4)
                pb = "ps%d" % (bank[0] % 3); bank[0] += 1
                mm([(R(pb, 0, (b1 - a1) * CH), B("id"), raw(a1, b1), True, False)] +
                   [(R(pb, j * CH, (j + 1) * CH), B("nid"), z, False, j == b1 - a1 - 1) for j in range(b1 - a1)])
                act(dst(a1, b1), R(pb, 0, (b1 - a1) * CH), ACT.Abs, scale=2.0)
        mm([(R("pd", 0, NP), B("id"), B("cx"), True, False), (R("pd", 0, NP), B("i4"), B("frac_" + s, 0, NP), False, False)])
        mm([(R(pu, 0, NP), B("id"), B("cy"), True, False),
            (R(pu, 0, 56), B("i8"), B("frac_" + s, 56, NP), False, False), (R(pu, 56, NP), B("i8"), B("frac_" + s, 0, 56), False, False)])
        for lo in range(0, 14, RG):
            hi = lo + RG
            for a, b in runs(xt, "d", GS, lo, hi): dblock(0, a, b, xr, wx)
            for a, b in runs(xt, "b", 7, lo, hi):
                vblock(0, a, b, xr)
                act(wx(a, b), xr(a, b), ACT.Abs, scale=2.0)
            mm([(R("pd", 8 * lo, 8 * hi), seln(i), wx(lo, hi, 16, i), False, hi == 14 and i == 15) for i in range(16)])
        if WPE:
            act(F("ww_" + s), R("pd", 0, NP), ACT.Identity, bias=F("bw_" + s, t, t + 1), scale=-1.0)
            mm([(R(pu, 0, 56), F("if32"), F("ww_" + s, 56, NP), False, False), (R(pu, 56, NP), F("if32"), F("ww_" + s, 0, 56), False, False)])
        for h in range(0 if WPE else 2):
            act(F("ww_" + s, 56 * h, 56 * h + 56), R("pd", 56 - 56 * h, NP - 56 * h), ACT.Identity, bias=F("bw_" + s, t, t + 1), scale=-1.0)
        act(F("vk_" + s), R("pd", 0, NP), ACT.Identity, bias=4130688.0 / 16777216.0, scale=1.0 / 16777216.0)
        for lo in range(0, 14, RG):
            hi = lo + RG
            for a, b in runs(yt, "d", GS, lo, hi): dblock(1, a, b, wy, ya)
            for a, b in runs(yt, "ab", 7, lo, hi):
                vblock(1, a, b, wy)
                if yt[a] == "a": ts(ya(a, b), wy(a, b), 0.0, 4.0, ALU.max, ALU.mult)
                else: act(ya(a, b), wy(a, b), ACT.Abs, scale=2.0)
            for a, b in runs(yt, "a", 14, lo, hi):
                mm([(R(pu, 8 * a, 8 * b), selp(i), wy(a, b, 16, i), False, False) for i in range(16)])
            mm([(R(pu, 8 * lo, 8 * hi), seln(i), ya(lo, hi, 16, i), False, hi == 14 and i == 15) for i in range(16)])

    def choose(t, c):
        s = str(c); wn = "win" + s
        K = lambda a=0, b=NP: F("kk_" + s, a, b)
        mx = F("mx_" + s)
        if not WPE: tt(R("pu" + s, 0, NP), R("pu" + s, 0, NP), F("ww_" + s), ALU.add)
        tt(K(), R("pu" + s, 0, NP), F("vk_" + s), ALU.max)
        tt(F("t1_" + s), K(0, 56), K(56, NP), ALU.max)
        tt(F("t2_" + s), F("t1_" + s, 0, 32), F("t1_" + s, 24, 56), ALU.max)
        tt(F("t3_" + s), F("t2_" + s, 0, 16), F("t2_" + s, 16, 32), ALU.max)
        tt(mx, F("t3_" + s, 0, 8), F("t3_" + s, 8, 16), ALU.max)
        rk[0] = 10 * t + 5 * c + RANK["n"]
        count(t, c)
        rk[0] = 10 * t + 5 * c + RANK["u"]
        update(t, c)
        rk[0] = 10 * t + 5 * c + RANK["c"]
        ts(F("aa_" + s), mx, 16777216.0, 4194304.0, ALU.mult, ALU.min)
        tt(I("m_" + s), F("aa_" + s), mx, ALU.add)
        ts(I("cd_" + s, 0, 8), I("m_" + s), 255, None, ALU.bitwise_and)
        nd_ = YT[c].count("d")
        if nd_ == 14:
            tt(I("cd_" + s, 8, 16), mx, ix(9, 17), ALU.min)
        elif nd_:
            tt(I("o2_" + s), mx, ix(9, 17), ALU.min)
            ts(F("fl_" + s), I("cd_" + s, 0, 8), float(CY + 8 * nd_), -8.0, ALU.is_ge, ALU.mult)
            tt(I("cd_" + s, 8, 16), I("o2_" + s), F("fl_" + s), ALU.add)
        else:
            tt(I("cd_" + s, 8, 16), mx, ix(1, 9), ALU.min)
        ts(U("o_" + s), I("cd_" + s), 16.0, KCOL, ALU.mult, ALU.add)
        if ON["t2"][c] == "S": act(B("t2_" + s), ind(R(wn, 0, 272), U("o_" + s, 8, 16)), ACT.Copy)
        else: cp(B("t2_" + s), ind(R(wn, 0, 272), U("o_" + s, 8, 16)))
        tt(B("s_" + s), ind(R(wn, 0, WINW), U("o_" + s, 0, 8)), B("t2_" + s), ALU.add)
        lin(ON["zp"][c], B("zp_" + s), B("s_" + s), 0.5, 63.875)
        lin(ON["zout"][c], zout(t, c), B("zp_" + s), 1.0, -128.0)
        send(zin(t + 1, c), zout(t, c), rank + 1 if t < TS - 1 else rank - (TS - 1))
        rk[0] = 10 * t + 5 * c + RANK["w"]
        if USCAN:
            pq = R("pz", 256, 384)
            mm([(pq, B("id"), B("dg"), True, False), (pq, B("bm"), B("zp_" + s), False, True)])
            add("V", lambda: g.vector.tensor_tensor_scan(A(F("ta_" + s)), A(F("rs")), A(pq), 0.0, ALU.mult, ALU.max),
                [F("ta_" + s)], [F("rs"), pq], CH * CYC)
            cp(I("ui_" + s), F("ta_" + s, 15, CH, 16))
        else:
            mm([(R("pz", 0, 8), selp(i), B("zp_" + s, i, CH, 16), i == 0, i == 15) for i in range(16)])
            ts(I("ui_" + s), R("pz", 0, 8), 1.0 / 4096, None, ALU.mult)
        ts(I("u15_" + s), I("ui_" + s), 15, None, ALU.bitwise_and)
        tt(F("cu_" + s), I("u15_" + s), F("ctile"), ALU.add)
        cp(U("c_" + s, 0, 8), F("cu_" + s))
        tt(B("xo_" + s), ind(XW(c), U("c_" + s, 0, 8)), B("zp_" + s), ALU.add)
        lin(ON["rr"][c], B("rr_" + s, 0, CH), B("xo_" + s), 0.5, 127.875)
        mm([(R("pz", 8, 16), F("sw32"), F("cu_" + s), True, True)])
        cp(U("c_" + s, 8, 16), R("pz", 8, 16))
        mm([(R("pz", 128, 256), B("sw"), B("rr_" + s, 0, CH), True, True)])
        act(B("rr_" + s, CH, 2 * CH), R("pz", 128, 256), ACT.Identity)
        tt(ind(XW(c), U("c_" + s)), B("rr_" + s), B("m192"), ALU.add)
        if t == TS - 1:
            x = T["X" + s]
            dma("Y", T.yx[64 * c:64 * c + 64, 0:2048], x[0:64, 0:2048], [], [XW(c)], 524288)
            dma("S" if c else "Y", T.yx[64 * c:64 * c + 64, 2048:4096], x[64:128, 2048:4096], [], [XW(c)], 524288)

    def update(t, c):
        s = str(c); mx = F("mx_" + s); K = F("kk_" + s)
        ts(F("mxe_" + s), mx, 0.5, None, ALU.min)
        tt(F("mm_" + s, 0, NP), ind(mx, U("lbc", 0, 7)), K, ALU.is_equal)
        tt(F("s1_" + s), ind(F("mxe_" + s), U("lbc", 0, 7)), K, ALU.is_equal)
        dl = lambda a, b, st=1: F("dl_" + s, a, b, st)
        tt(dl(0, 224, 2), F("mm_" + s, 0, NP), F("gg_" + s, 0, 224, 2), ALU.mult)
        tt(dl(1, 112, 2), F("s1_" + s, 56, NP), F("gg_" + s, 1, 112, 2), ALU.mult)
        tt(dl(113, 224, 2), F("s1_" + s, 0, 56), F("gg_" + s, 113, 224, 2), ALU.mult)
        d1 = lambda a, b, st=1: F("d1_" + s, a, b, st)
        tt(d1(0, 112), dl(0, 112), dl(112, 224), ALU.add)
        tt(d1(0, 48), d1(0, 48), d1(64, 112), ALU.add)
        tt(d1(0, 32), d1(0, 32), d1(32, 64), ALU.add)
        tt(d1(0, 16), d1(0, 16), d1(16, 32), ALU.add)
        tt(stout(t, c, 112, 120), stin(t, c, 112, 120), d1(0, 16, 2), ALU.subtract)
        tt(stout(t, c, 120, 128), stin(t, c, 120, 128), d1(1, 16, 2), ALU.subtract)
        tt(F("mm_" + s, NP, 224), stin(t, c, 0, NP), dl(0, 224, 2), ALU.add)
        tt(stout(t, c, 0, NP), F("mm_" + s, NP, 224), dl(1, 224, 2), ALU.add)
        send(stin(t + 1, c), stout(t, c), rank + 1 if t < TS - 1 else rank - (TS - 1))

    def count(t, c):
        s = str(c)
        TC, R1, NRR, AN, BT, AB = [cs(c, j) for j in range(6)]
        pc = R("pz", 16, 24)
        act(B("sg_" + s), F("mx_" + s), ACT.Sign, bias=-0.5)
        mm([(pc, B("bm2"), B("sg_" + s), True, True)])
        act(F("junk_" + s), pc, ACT.Identity, bias=16.0, scale=-0.5, acc=F("ye_" + s, t, t + 1))
        if t < TS - 1:
            ts(TC, F("ye_" + s, t, t + 1), AB, -31.5 - AB0, ALU.add, ALU.add)
            ts(R1, TC, M29, -M29, ALU.add, ALU.add)
            ts(AB, TC, R1, 31.5 + AB0, ALU.subtract, ALU.add)
        else:
            a = _F["ye_" + s][0]
            dma("Y", T.ye[64 * c:64 * c + 64, :], T.FF[0:64, a:a + TS], [], [F("ye_" + s)], 1536)

    def lut():
        ts(F("e1"), F("hi"), KCOL, None, ALU.is_equal)
        ts(F("e2"), F("lo"), KCOL, None, ALU.is_equal)
        tt(B("lt", 0, 256), F("e1"), F("lo"), ALU.mult)
        tt(B("lt", 256, 512), F("e2"), F("hi"), ALU.mult)
        tt(B("lut", 0, 256), B("lt", 0, 256), B("lt", 256, 512), ALU.add)
        tt(B("lt", 0, 256), F("e1"), F("e2"), ALU.add)
        ts(B("lut", 256, 512), B("lt", 0, 256), KCOL, None, ALU.mult)
        act(B("lut", 512, 768), F("hi"), ACT.Identity)

    def finish(c):
        s = str(c)
        store2("YY", T.yz, c, zin(TS, c), 16384)
        unpack(TS, c, CH)
        act(F("f16_" + s), B("frac_" + s), ACT.Identity, scale=16.0)
        tt(F("pc_" + s, 0, 56), F("f16_" + s, 0, 56), B("frac_" + s, 56, NP), ALU.add)
        tt(F("pc_" + s, 56, 64), F("f16_" + s, 112, 120), B("frac_" + s, 120, 128), ALU.add)
        ts(U("fo_" + s, 0, 56), F("pc_" + s, 0, 56), 16.0, 127.5, ALU.mult, ALU.add)
        ts(U("fo_" + s, 56, 64), F("pc_" + s, 56, 64), 16.0, 383.5, ALU.mult, ALU.add)
        ts(U("fo_" + s, 64, 72), F("pc_" + s, 56, 64), 16.0, 639.5, ALU.mult, ALU.add)
        L = B("lut")
        cp(B("xr_" + s, 0, 512), ind(L, U("fo_" + s, 0, 32)))
        act(B("xr_" + s, 512, 1024), ind(L, U("fo_" + s, 32, 64)), ACT.Copy)
        cp(F("yfo_" + s), ind(L, U("fo_" + s, 64, 72)))
        pb = R("pu" + s, 0, CH)
        mm([(pb, B("id"), B("xr_" + s, j * CH, (j + 1) * CH), j == 0, j == 7) for j in range(8)])
        act(F("yp_" + s), pb, ACT.Identity)
        store2("SY", T.yp, c, F("yp_" + s), 32768)
        a = _F["yfo_" + s][0]
        for h in range(2):
            dma("Y", T.yf[4 * c:4 * c + 4, h * CH:(h + 1) * CH], T.FF[64 * h:64 * h + 64:16, a:a + CH], [], [F("yfo_" + s)], 2048)

    rk[0] = -50; arrange(0)
    rk[0] = RANK["a1"]; arrange(1)
    rk[0] = RANK["l"]; lut()
    for t in range(TS):
        for c in range(2):
            for f, k in ((index, "i"), (gathers, "g"), (choose, "c")):
                rk[0] = 10 * t + 5 * c + RANK[k]; f(t, c)
    for c in range(2):
        rk[0] = 10 * (TS - 1) + 5 * c + RANK["w"] + RANK["f"]; finish(c)
    return ops


def depend(ops):
    last = {}
    for n, o in enumerate(ops):
        deps = set()
        for keys, w in ((o["rd"], False), (o["wr"], True)):
            for name, lo, hi in keys:
                for m, a, b, ww in last.get(name, []):
                    if a < hi and lo < b and (w or ww): deps.add(m)
        if o["par"]:
            deps.discard(n - 1)
        else:
            for name, lo, hi in o["wr"]:
                last[name] = [e for e in last.get(name, []) if not (lo <= e[1] and e[2] <= hi)]
        for keys, w in ((o["rd"], False), (o["wr"], True)):
            for e in set(keys):
                last.setdefault(e[0], []).append((n, e[1], e[2], w))
        deps.discard(n)
        o["deps"] = sorted(deps)


def order(ops):
    n = len(ops)
    users = [[] for o in ops]
    for j, o in enumerate(ops):
        for d in o["deps"]: users[d].append(j)
    pri = [0.0] * n
    for j in range(n - 1, -1, -1):
        pri[j] = ops[j]["lat"] + max([pri[u] + WAKE for u in users[j]] + [0.0])
    left = [len(o["deps"]) for o in ops]
    rdy = [0.0] * n
    free = {q: 0.0 for q in "VSPGY"}
    cand = {q: [] for q in "VSPGY"}
    for j, o in enumerate(ops):
        if left[j] == 0: cand[o["q"]].append(j)
    seq = []
    while len(seq) < n:
        best = None
        for q in cand:
            if cand[q]:
                e = max(free[q], min(rdy[j] for j in cand[q]))
                if best is None or e < best[0]: best = (e, q)
        e, q = best
        j = max((j for j in cand[q] if rdy[j] <= e + 50.0), key=lambda j: (-ops[j]["rank"], pri[j], -j))
        cand[q].remove(j)
        st = max(free[q], rdy[j]); free[q] = st + ops[j]["occ"]
        ops[j]["start"] = st; seq.append(j)
        for u in users[j]:
            pp = ops[j]["q"] == "P" and ops[u]["q"] == "P"
            rdy[u] = max(rdy[u], st + (ops[j]["occ"] if pp else ops[j]["lat"] + WAKE))
            left[u] -= 1
            if left[u] == 0: cand[ops[u]["q"]].append(u)
    return seq


def rank_program(g, core, T, topo):
    if T.rank_of(core) is None:
        return
    ops = build(g, core, T, topo)
    depend(ops)
    seq = order(ops)
    queue = {"V": g.vector, "S": g.scalar, "P": g.tensor, "G": g, "Y": g.sync}
    csem = {"V": T.sem.cV, "S": T.sem.cS, "P": T.sem.cP, "G": T.sem.cG}
    cnt = {q: 0 for q in csem}
    seen = {q: {} for q in queue}
    sent = 0
    for j in seq:
        o = ops[j]; q = o["q"]
        need = {}
        for d in o["deps"]:
            p = ops[d]
            if p["kind"] == "c":
                if p["q"] == "P" and q == "P": continue
                key, sem, val = p["q"], csem[p["q"]], p["num"]
            else:
                key, sem, val = d, p["sem"][0], p["sem"][1]
            if val > need.get(key, (None, 0))[1]: need[key] = (sem, val)
        for key, (sem, val) in need.items():
            if seen[q].get(key, 0) < val:
                queue[q].wait_ge(sem, val); seen[q][key] = val
        r = o["fn"]()
        if o["kind"] == "c":
            cnt[q] += 1; o["num"] = cnt[q]; r.then_inc(csem[q], 1)
        elif o["kind"] == "d":
            r.then_inc(o["sem"][0], 16)
        else:
            sent += o["sem"][1]
    for q in csem:
        g.wait_ge(csem[q], cnt[q])
    for o in ops:
        if o["kind"] != "c": g.wait_ge(o["sem"][0], o["sem"][1])
    g.wait_ge(T.sem.sent, sent)
